import numpy as np
import ml_dtypes


def mxq(x, axis, fmt="e4m3"):
    dtype, down = {"e4m3": (ml_dtypes.float8_e4m3fn, 7), "e5m2": (ml_dtypes.float8_e5m2, 14)}[fmt]
    v = np.moveaxis(np.asarray(x, np.float32).astype(ml_dtypes.bfloat16).astype(np.float64), axis, -1)
    blocks = v.reshape(v.shape[:-1] + (-1, 32))
    amax = np.abs(blocks).max(-1, keepdims=True)
    byte = np.maximum(np.where(amax > 0, np.frexp(amax)[1] - 1 + 127, 0) - down, 1)
    scale = np.exp2(byte - 127.0)
    codes = (blocks / scale).astype(np.float32).astype(dtype).astype(np.float64)
    return np.moveaxis((codes * scale).reshape(v.shape), -1, axis)


WIDE = False


def mx_kscale(k):
    if not WIDE:
        return np.ones(k)
    levels = np.array([18, -18])
    if k % 512:
        return np.exp2(np.random.permutation(np.resize(levels, k // 32))).repeat(32)
    a = np.empty((k // 512, 16))
    for p in range(k // 512):
        a[p, :8] = np.random.permutation(np.resize(levels, 8))
        for g in range(8):
            far = levels[np.abs(levels - a[p, g]) >= 10]
            a[p, g + 8] = far[np.random.randint(len(far))]
    return np.exp2(a.ravel()).repeat(32)


def f64(x):
    return np.asarray(x).astype(np.float64)


def striped(idx):
    return np.tile(np.asarray(idx).reshape(-1, 16).T, (8, 1)).astype(np.uint16)


def unstriped(offs):
    return offs[:16].T.reshape(-1).astype(np.int64)


V, E, D, DV = 1024, 2048, 256, 512


def setup_inputs():
    n = np.random.standard_normal
    u = mx_kscale(E)
    coarse = lambda x: x.astype(np.float32).astype(ml_dtypes.bfloat16).astype(np.float64)
    return {
        "xT": (coarse(n((D, V)))).astype(np.float32),
        "dyT": (coarse(n((DV, V)))).astype(np.float32),
        "hE": (np.random.randint(1, 32, (DV, E)) / 32.0).astype(np.float32),
        "sw": np.tile(np.random.randint(8, 33, E) / 512.0 / u, (128, 1)).astype(np.float32),
        "tw": np.tile(np.random.randint(8, 33, E) / 16.0 * u, (128, 1)).astype(np.float32),
        "offs": striped(np.random.randint(0, V, E)),
        "offs2": striped(np.random.randint(0, V, E)),
    }


def reference(xT, dyT, hE, sw, tw, offs, offs2):
    h = f64(hE)
    xe = f64(sw)[:1] * f64(xT)[:, unstriped(offs)]
    dz = f64(tw)[:1] * f64(dyT)[:, unstriped(offs2)] * h * (1.0 - h)
    return mxq(xe, 1, "e4m3") @ mxq(dz, 1, "e5m2").T

@@ -1,0 +1,164 @@
+from contextlib import ExitStack
+
+import concourse.mybir as mybir
+from concourse.masks import make_identity
+
+V, E, D, DV = 1024, 2048, 256, 512
+FLOPS = 2 * D * DV * E
+
+F32 = mybir.dt.float32
+BF16 = mybir.dt.bfloat16
+U32 = mybir.dt.uint32
+U16 = mybir.dt.uint16
+U8 = mybir.dt.uint8
+E4M3 = mybir.dt.float8_e4m3fn_x4
+E5M2 = mybir.dt.float8_e5m2_x4
+ACT = mybir.ActivationFunctionType
+ALU = mybir.AluOpType
+
+P = 128
+PACK = 4
+K_PASS = P * PACK
+PASSES = E // K_PASS
+LIST_COLS = K_PASS // 16
+X_BLOCKS = D // P
+DY_BLOCKS = DV // P
+
+
+def tile_attend_gmw_sig_kernel(tc, xT, dyT, hE, sw, tw, offs, offs2, out):
+    nc = tc.nc
+    with ExitStack() as ctx:
+        keep = ctx.enter_context(tc.tile_pool(name="keep", bufs=1))
+        ring = ctx.enter_context(tc.tile_pool(name="ring", bufs=2))
+        small = ctx.enter_context(tc.tile_pool(name="small", bufs=4))
+        turn = ctx.enter_context(tc.psum_pool(name="turn", bufs=6))
+        sums = ctx.enter_context(tc.psum_pool(name="sums", bufs=1))
+
+        src = keep.tile([P, E // 16], U16, name="src")
+        dst = keep.tile([P, E // 16], U16, name="dst")
+        x_tab = [keep.tile([P, V], F32, name="x_tab%d" % b) for b in range(X_BLOCKS)]
+        dy_tab = [keep.tile([P, V], F32, name="dy_tab%d" % b) for b in range(DY_BLOCKS)]
+        h_in = [keep.tile([P, E], F32, name="h_in%d" % b) for b in range(DY_BLOCKS)]
+        sw_in = [keep.tile([P, K_PASS], F32, name="sw_in%d" % g) for g in range(PASSES)]
+        tw_in = [keep.tile([P, K_PASS], F32, name="tw_in%d" % g) for g in range(PASSES)]
+        ident = keep.tile([P, P], F32, name="ident")
+        x_codes = [[keep.tile([P, P], U32, name="x_codes%d_%d" % (b, g), align_bytes=64) for g in range(PASSES)] for b in range(X_BLOCKS)]
+        x_scales = [[keep.tile([P, P], U8, name="x_scales%d_%d" % (b, g), align_bytes=64) for g in range(PASSES)] for b in range(X_BLOCKS)]
+        dz_codes = [keep.tile([P, DV], U32, name="dz_codes%d" % g, align_bytes=64) for g in range(PASSES)]
+        dz_scales = [keep.tile([P, DV], U8, name="dz_scales%d" % g, align_bytes=64) for g in range(PASSES)]
+        acc = [sums.tile([P, DV], F32, name="acc%d" % b) for b in range(X_BLOCKS)]
+
+        def edges(g):
+            return slice(g * K_PASS, (g + 1) * K_PASS)
+
+        def entries(g):
+            return slice(g * LIST_COLS, (g + 1) * LIST_COLS)
+
+        def rows(b):
+            return slice(b * P, (b + 1) * P)
+
+        nc.sync.dma_start(src[:], offs)
+        nc.sync.dma_start(x_tab[0][:], xT[rows(0), :])
+        for g in range(PASSES):
+            nc.sync.dma_start(sw_in[g][:], sw[:, edges(g)])
+        nc.sync.dma_start(dst[:], offs2)
+        nc.sync.dma_start(dy_tab[0][:], dyT[rows(0), :])
+        for g in range(PASSES):
+            nc.sync.dma_start(tw_in[g][:], tw[:, edges(g)])
+        for b in range(DY_BLOCKS):
+            nc.sync.dma_start(h_in[b][:], hE[rows(b), :])
+            if b + 1 < DY_BLOCKS:
+                nc.sync.dma_start(dy_tab[b + 1][:], dyT[rows(b + 1), :])
+        nc.sync.dma_start(x_tab[1][:], xT[rows(1), :])
+
+        make_identity(nc, ident[:])
+
+        def x_gather(b, g):
+            xe = small.tile([P, K_PASS], F32, name="xe")
+            nc.vector.tensor_tensor(xe[:], x_tab[b][:].indirect(src[:, entries(g)]), sw_in[g][:], ALU.mult)
+            bank = turn.tile([P, PACK, P], F32, name="bank")
+            for t in range(PACK):
+                nc.tensor.transpose(bank[:, t, :], xe[:, t:K_PASS:PACK], ident[:])
+            woven = small.tile([P, P, PACK], BF16, name="x_woven", align_bytes=64)
+            nc.scalar.copy(woven[:], bank[:].rearrange("p t d -> p d t"))
+            return woven
+
+        def x_quantise(b, g, woven):
+            nc.vector.quantize_mx(
+                out=x_codes[b][g][:].bitcast(E4M3),
+                scales=x_scales[b][g][:],
+                in_=woven[:].rearrange("p d t -> p (d t)"),
+            )
+
+        def dy_gather(b):
+            weighted = ring.tile([P, E], F32, name="weighted")
+            for g in range(PASSES):
+                nc.vector.tensor_tensor(weighted[:, edges(g)], dy_tab[b][:].indirect(dst[:, entries(g)]), tw_in[g][:], ALU.mult)
+            centred = ring.tile([P, E], F32, name="centred")
+            nc.scalar.activation(centred[:], h_in[b][:], ACT.Square, bias=-0.5, scale=1.0)
+            return weighted, centred
+
+        def dz_form(weighted, centred):
+            dz = ring.tile([P, E], BF16, name="dz")
+            nc.vector.scalar_tensor_tensor(dz[:], centred[:], 0.25, weighted[:], ALU.subtract, ALU.mult)
+            words = dz[:].bitcast(F32)
+            woven_pairs = []
+            for half in range(PASSES // 2):
+                bank = turn.tile([P, 2, 2, P], F32, name="bank")
+                for j in range(2):
+                    g = 2 * half + j
+                    for u in range(2):
+                        nc.tensor.transpose(bank[:, j, u, :], words[:, 256 * g + u : 256 * (g + 1) : 2], ident[:])
+                woven = small.tile([P, 2, K_PASS], BF16, name="dz_woven", align_bytes=64)
+                nc.scalar.copy(
+                    woven[:].bitcast(F32).rearrange("p j (n u) -> p j n u", u=2),
+                    bank[:].rearrange("p j u n -> p j n u"),
+                )
+                woven_pairs.append(woven)
+            return woven_pairs
+
+        def dz_quantise(b, woven_pairs):
+            for g in range(PASSES):
+                nc.vector.quantize_mx(
+                    out=dz_codes[g][:, rows(b)].bitcast(E5M2),
+                    scales=dz_scales[g][:, rows(b)],
+                    in_=woven_pairs[g // 2][:, g % 2, :],
+                )
+
+        def product(b, g):
+            nc.tensor.matmul_mx(
+                out=acc[b][:],
+                lhsT=x_codes[b][g][:].bitcast(E4M3),
+                lhsT_scale=x_scales[b][g][:],
+                rhs=dz_codes[g][:].bitcast(E5M2),
+                rhs_scale=dz_scales[g][:],
+                start=(g == 0),
+                stop=(g == PASSES - 1),
+            )
+
+        def store(b):
+            result = ring.tile([P, DV], F32, name="result")
+            nc.scalar.activation(result[:], acc[b][:], ACT.Copy, scale=-1.0)
+            nc.sync.dma_start(out[rows(b), :], result[:])
+
+        x_first = [x_gather(0, g) for g in range(PASSES)]
+        factors = dy_gather(0)
+        for g in range(PASSES):
+            x_quantise(0, g, x_first[g])
+        pending = None
+        for b in range(DY_BLOCKS):
+            following = dy_gather(b + 1) if b + 1 < DY_BLOCKS else None
+            if pending is not None:
+                dz_quantise(b - 1, pending)
+            pending = dz_form(*factors)
+            factors = following
+        x_last = [x_gather(1, g) for g in range(2)]
+        dz_quantise(DY_BLOCKS - 1, pending)
+        for g in range(PASSES):
+            product(0, g)
+        store(0)
+        x_last.extend(x_gather(1, g) for g in range(2, PASSES))
+        for g in range(PASSES):
+            x_quantise(1, g, x_last[g])
+            product(1, g)
+        store(1)

@@ -23,30 +23,45 @@ PASSES = E // K_PASS
 LIST_COLS = K_PASS // 16
 X_BLOCKS = D // P
 DY_BLOCKS = DV // P
+HALF = E // 2
+CHUNKS = K_PASS // P
+RING = 5
 
 
 def tile_attend_gmw_sig_kernel(tc, xT, dyT, hE, sw, tw, offs, offs2, out):
     nc = tc.nc
     with ExitStack() as ctx:
         keep = ctx.enter_context(tc.tile_pool(name="keep", bufs=1))
-        ring = ctx.enter_context(tc.tile_pool(name="ring", bufs=2))
-        small = ctx.enter_context(tc.tile_pool(name="small", bufs=4))
-        turn = ctx.enter_context(tc.psum_pool(name="turn", bufs=6))
-        sums = ctx.enter_context(tc.psum_pool(name="sums", bufs=1))
+        psum = ctx.enter_context(tc.psum_pool(name="psum", bufs=1))
 
         src = keep.tile([P, E // 16], U16, name="src")
         dst = keep.tile([P, E // 16], U16, name="dst")
         x_tab = [keep.tile([P, V], F32, name="x_tab%d" % b) for b in range(X_BLOCKS)]
         dy_tab = [keep.tile([P, V], F32, name="dy_tab%d" % b) for b in range(DY_BLOCKS)]
-        h_in = [keep.tile([P, E], F32, name="h_in%d" % b) for b in range(DY_BLOCKS)]
-        sw_in = [keep.tile([P, K_PASS], F32, name="sw_in%d" % g) for g in range(PASSES)]
-        tw_in = [keep.tile([P, K_PASS], F32, name="tw_in%d" % g) for g in range(PASSES)]
+        h_early = [keep.tile([P, HALF], F32, name="h_early%d" % b) for b in range(DY_BLOCKS)]
+        h_late = {(g, j): keep.tile([P, 2, K_PASS], F32, name="h_late%d_%d" % (g, j)) for g in (2, 3) for j in range(2)}
+        sw_first = [keep.tile([P, K_PASS // 2], F32, name="sw_first%d" % j) for j in range(2)]
+        sw_in = {g: keep.tile([P, K_PASS], F32, name="sw_in%d" % g) for g in range(1, PASSES)}
+        tw_in = [keep.tile([P, K_PASS], F32, name="tw_in%d" % g) for g in range(2)]
+        tw_rows = keep.tile([P, P], F32, name="tw_rows")
+        tw_col = keep.tile([P, 8], F32, name="tw_col")
+        tw_bias = keep.tile([P, 8], F32, name="tw_bias")
         ident = keep.tile([P, P], F32, name="ident")
-        x_codes = [[keep.tile([P, P], U32, name="x_codes%d_%d" % (b, g), align_bytes=64) for g in range(PASSES)] for b in range(X_BLOCKS)]
-        x_scales = [[keep.tile([P, P], U8, name="x_scales%d_%d" % (b, g), align_bytes=64) for g in range(PASSES)] for b in range(X_BLOCKS)]
-        dz_codes = [keep.tile([P, DV], U32, name="dz_codes%d" % g, align_bytes=64) for g in range(PASSES)]
-        dz_scales = [keep.tile([P, DV], U8, name="dz_scales%d" % g, align_bytes=64) for g in range(PASSES)]
-        acc = [sums.tile([P, DV], F32, name="acc%d" % b) for b in range(X_BLOCKS)]
+        gathered = [keep.tile([P, K_PASS], F32, name="gathered%d" % i) for i in range(10)]
+        dz_early = [keep.tile([P, HALF], BF16, name="dz_early%d" % b) for b in range(DY_BLOCKS)]
+        banks = [psum.tile([P, PACK, P], F32, name="bank%d" % i) for i in range(RING)]
+        acc = [psum.tile([P, DV], F32, name="acc%d" % b) for b in range(X_BLOCKS)]
+        weighted = [keep.tile([P, HALF], F32, name="weighted%d" % b) for b in range(DY_BLOCKS)]
+        centred = [keep.tile([P, HALF], F32, name="centred%d" % b) for b in range(DY_BLOCKS)]
+        centred_late = {(g, j): keep.tile([P, 2, K_PASS], F32, name="centred_late%d_%d" % (g, j)) for g in (2, 3) for j in range(2)}
+        factor_t = {(g, j, c): keep.tile([P, 2 * P], F32, name="factor_t%d_%d_%d" % (g, j, c)) for g in (2, 3) for j in range(2) for c in range(CHUNKS)}
+        factor = {(g, b): keep.tile([P, K_PASS], F32, name="factor%d_%d" % (g, b)) for g in (2, 3) for b in range(DY_BLOCKS)}
+        x_woven = [keep.tile([P, PASSES, K_PASS], BF16, name="x_woven%d" % b, align_bytes=64) for b in range(X_BLOCKS)]
+        x_codes = [keep.tile([P, PASSES * P], U32, name="x_codes%d" % b, align_bytes=64) for b in range(X_BLOCKS)]
+        x_scales = [keep.tile([P, PASSES * P], U8, name="x_scales%d" % b, align_bytes=64) for b in range(X_BLOCKS)]
+        dz_woven = [keep.tile([P, 2, DV * PACK], BF16, name="dz_woven%d" % j, align_bytes=64) for j in range(2)]
+        dz_codes = [keep.tile([P, 2 * DV], U32, name="dz_codes%d" % j, align_bytes=64) for j in range(2)]
+        dz_scales = [keep.tile([P, 2 * DV], U8, name="dz_scales%d" % j, align_bytes=64) for j in range(2)]
 
         def edges(g):
             return slice(g * K_PASS, (g + 1) * K_PASS)
@@ -57,108 +72,234 @@ def tile_attend_gmw_sig_kernel(tc, xT, dyT, hE, sw, tw, offs, offs2, out):
         def rows(b):
             return slice(b * P, (b + 1) * P)
 
+        def load_h_late(g, j):
+            nc.sync.dma_start(h_late[g, j][:], hE[2 * j * P : 2 * (j + 1) * P, edges(g)].rearrange("(b p) e -> p b e", p=P))
+
+        def load_h_early(b):
+            nc.sync.dma_start(h_early[b][:], hE[rows(b), 0:HALF])
+
+        def load_dy(b):
+            nc.sync.dma_start(dy_tab[b][:], dyT[rows(b), :])
+
+        nc.gpsimd.memset(tw_rows[:], 0.0)
+        make_identity(nc, ident[:])
         nc.sync.dma_start(src[:], offs)
         nc.sync.dma_start(x_tab[0][:], xT[rows(0), :])
-        for g in range(PASSES):
-            nc.sync.dma_start(sw_in[g][:], sw[:, edges(g)])
+        for j in range(2):
+            nc.sync.dma_start(sw_first[j][:], sw[:, j * K_PASS // 2 : (j + 1) * K_PASS // 2])
+        nc.sync.dma_start(sw_in[1][:], sw[:, edges(1)])
+        nc.scalar.dma_start(tw_rows[0:8, :], tw[0:1, HALF:E].rearrange("o (c p) -> (o c) p", p=P))
+        load_h_late(2, 0)
+        nc.sync.dma_start(sw_in[2][:], sw[:, edges(2)])
+        nc.sync.dma_start(sw_in[3][:], sw[:, edges(3)])
         nc.sync.dma_start(dst[:], offs2)
-        nc.sync.dma_start(dy_tab[0][:], dyT[rows(0), :])
-        for g in range(PASSES):
-            nc.sync.dma_start(tw_in[g][:], tw[:, edges(g)])
-        for b in range(DY_BLOCKS):
-            nc.sync.dma_start(h_in[b][:], hE[rows(b), :])
-            if b + 1 < DY_BLOCKS:
-                nc.sync.dma_start(dy_tab[b + 1][:], dyT[rows(b + 1), :])
+        load_dy(0)
+        nc.sync.dma_start(tw_in[0][:], tw[:, edges(0)])
+        nc.sync.dma_start(tw_in[1][:], tw[:, edges(1)])
+        load_dy(1)
+        load_h_late(2, 1)
+        load_h_late(3, 0)
+        load_dy(2)
+        load_h_late(3, 1)
+        load_h_early(0)
+        load_dy(3)
+        load_h_early(1)
+        load_h_early(2)
+        load_h_early(3)
         nc.sync.dma_start(x_tab[1][:], xT[rows(1), :])
 
-        make_identity(nc, ident[:])
+        used = []
+
+        def next_bank():
+            used.append(None)
+            return banks[(len(used) - 1) % RING]
+
+        def gather(unit, table, offsets, g, scales):
+            width = K_PASS // len(scales)
+            for j, scale in enumerate(scales):
+                first = g * LIST_COLS + j * width // 16
+                nc.vector.tensor_tensor(
+                    unit[:, j * width : (j + 1) * width], table[:].indirect(offsets[:, first : first + width // 16]), scale[:], ALU.mult
+                )
+
+        def weave(unit, target):
+            bank = next_bank()
+            for t in range(PACK):
+                nc.tensor.transpose(bank[:, t, :], unit[:, t:K_PASS:PACK], ident[:])
+            nc.scalar.copy(target.rearrange("p (c t) -> p c t", t=PACK), bank[:].rearrange("p t c -> p c t"))
+
+        x_buf = {(0, 0): 0, (0, 1): 1, (0, 2): 2, (0, 3): 3, (1, 0): 2, (1, 1): 3, (1, 2): 1, (1, 3): 2}
+        dz_buf = {(0, 2): 0, (1, 2): 1, (2, 2): 2, (3, 2): 3, (0, 3): 0, (1, 3): 1, (2, 3): 2, (3, 3): 3}
 
         def x_gather(b, g):
-            xe = small.tile([P, K_PASS], F32, name="xe")
-            nc.vector.tensor_tensor(xe[:], x_tab[b][:].indirect(src[:, entries(g)]), sw_in[g][:], ALU.mult)
-            bank = turn.tile([P, PACK, P], F32, name="bank")
-            for t in range(PACK):
-                nc.tensor.transpose(bank[:, t, :], xe[:, t:K_PASS:PACK], ident[:])
-            woven = small.tile([P, P, PACK], BF16, name="x_woven", align_bytes=64)
-            nc.scalar.copy(woven[:], bank[:].rearrange("p t d -> p d t"))
-            return woven
+            gather(gathered[x_buf[b, g]], x_tab[b], src, g, sw_first if g == 0 else [sw_in[g]])
 
-        def x_quantise(b, g, woven):
+        def x_weave(b, g):
+            weave(gathered[x_buf[b, g]], x_woven[b][:, g, :])
+
+        def dz_gather(b, g):
+            gather(gathered[dz_buf[b, g]], dy_tab[b], dst, g, [factor[g, b]])
+
+        def dz_weave(b, g):
+            weave(gathered[dz_buf[b, g]], dz_woven[1][:, g - 2, b * K_PASS : (b + 1) * K_PASS])
+
+        def x_quantise(b, first, last):
             nc.vector.quantize_mx(
-                out=x_codes[b][g][:].bitcast(E4M3),
-                scales=x_scales[b][g][:],
-                in_=woven[:].rearrange("p d t -> p (d t)"),
+                out=x_codes[b][:, first * P : last * P].bitcast(E4M3),
+                scales=x_scales[b][:, first * P : last * P],
+                in_=x_woven[b][:, first:last, :].rearrange("p g c -> p (g c)"),
             )
 
+        def dz_quantise(j, first, last):
+            nc.vector.quantize_mx(
+                out=dz_codes[j][:, first * DV : last * DV].bitcast(E5M2),
+                scales=dz_scales[j][:, first * DV : last * DV],
+                in_=dz_woven[j][:, first:last, :].rearrange("p g c -> p (g c)"),
+            )
+
+        def tw_columns():
+            bank = next_bank()
+            nc.tensor.transpose(bank[:, 0, :], tw_rows[:], ident[:])
+            nc.scalar.copy(tw_col[:], bank[:, 0, 0:8])
+            nc.scalar.activation(tw_bias[:], bank[:, 0, 0:8], ACT.Copy, scale=-0.25)
+
+        def square_late(g, j):
+            nc.scalar.activation(centred_late[g, j][:], h_late[g, j][:], ACT.Square, bias=-0.5, scale=1.0)
+
+        def scale_late(g, j, half):
+            bank = next_bank()
+            for i in range(2):
+                for b in range(2):
+                    nc.tensor.transpose(bank[:, 2 * i + b, :], centred_late[g, j][:, b, rows(2 * half + i)], ident[:])
+            for i in range(2):
+                c = 2 * half + i
+                col = (g - 2) * CHUNKS + c
+                nc.scalar.activation(
+                    factor_t[g, j, c][:],
+                    bank[:, 2 * i : 2 * i + 2, :].rearrange("p b n -> p (b n)"),
+                    ACT.Identity,
+                    bias=tw_bias[:, col : col + 1],
+                    scale=tw_col[:, col : col + 1],
+                )
+
+        def turn_back(g, b):
+            bank = next_bank()
+            for c in range(CHUNKS):
+                nc.tensor.transpose(bank[:, c, :], factor_t[g, b // 2, c][:, rows(b % 2)], ident[:])
+            nc.scalar.copy(factor[g, b][:], bank[:].rearrange("p c e -> p (c e)"))
+
         def dy_gather(b):
-            weighted = ring.tile([P, E], F32, name="weighted")
-            for g in range(PASSES):
-                nc.vector.tensor_tensor(weighted[:, edges(g)], dy_tab[b][:].indirect(dst[:, entries(g)]), tw_in[g][:], ALU.mult)
-            centred = ring.tile([P, E], F32, name="centred")
-            nc.scalar.activation(centred[:], h_in[b][:], ACT.Square, bias=-0.5, scale=1.0)
-            return weighted, centred
+            for g in range(2):
+                nc.vector.tensor_tensor(weighted[b][:, edges(g)], dy_tab[b][:].indirect(dst[:, entries(g)]), tw_in[g][:], ALU.mult)
 
-        def dz_form(weighted, centred):
-            dz = ring.tile([P, E], BF16, name="dz")
-            nc.vector.scalar_tensor_tensor(dz[:], centred[:], 0.25, weighted[:], ALU.subtract, ALU.mult)
-            words = dz[:].bitcast(F32)
-            woven_pairs = []
-            for half in range(PASSES // 2):
-                bank = turn.tile([P, 2, 2, P], F32, name="bank")
-                for j in range(2):
-                    g = 2 * half + j
-                    for u in range(2):
-                        nc.tensor.transpose(bank[:, j, u, :], words[:, 256 * g + u : 256 * (g + 1) : 2], ident[:])
-                woven = small.tile([P, 2, K_PASS], BF16, name="dz_woven", align_bytes=64)
-                nc.scalar.copy(
-                    woven[:].bitcast(F32).rearrange("p j (n u) -> p j n u", u=2),
-                    bank[:].rearrange("p j u n -> p j n u"),
-                )
-                woven_pairs.append(woven)
-            return woven_pairs
+        def square_early(b):
+            nc.scalar.activation(centred[b][:], h_early[b][:], ACT.Square, bias=-0.5, scale=1.0)
 
-        def dz_quantise(b, woven_pairs):
-            for g in range(PASSES):
-                nc.vector.quantize_mx(
-                    out=dz_codes[g][:, rows(b)].bitcast(E5M2),
-                    scales=dz_scales[g][:, rows(b)],
-                    in_=woven_pairs[g // 2][:, g % 2, :],
-                )
+        def dz_form(b):
+            nc.vector.scalar_tensor_tensor(dz_early[b][:], centred[b][:], 0.25, weighted[b][:], ALU.subtract, ALU.mult)
 
-        def product(b, g):
+        def weave_words(b):
+            words = dz_early[b][:].bitcast(F32)
+            bank = next_bank()
+            for g in range(2):
+                for u in range(2):
+                    nc.tensor.transpose(bank[:, 2 * g + u, :], words[:, 256 * g + u : 256 * (g + 1) : 2], ident[:])
+            nc.scalar.copy(
+                dz_woven[0][:, :, b * K_PASS : (b + 1) * K_PASS].bitcast(F32).rearrange("p g (n u) -> p g n u", u=2),
+                bank[:].rearrange("p (g u) n -> p g n u", u=2),
+            )
+
+        def product(acc, b, g):
             nc.tensor.matmul_mx(
-                out=acc[b][:],
-                lhsT=x_codes[b][g][:].bitcast(E4M3),
-                lhsT_scale=x_scales[b][g][:],
-                rhs=dz_codes[g][:].bitcast(E5M2),
-                rhs_scale=dz_scales[g][:],
+                out=acc[:],
+                lhsT=x_codes[b][:, g * P : (g + 1) * P].bitcast(E4M3),
+                lhsT_scale=x_scales[b][:, g * P : (g + 1) * P],
+                rhs=dz_codes[g // 2][:, (g % 2) * DV : (g % 2 + 1) * DV].bitcast(E5M2),
+                rhs_scale=dz_scales[g // 2][:, (g % 2) * DV : (g % 2 + 1) * DV],
                 start=(g == 0),
                 stop=(g == PASSES - 1),
             )
 
-        def store(b):
-            result = ring.tile([P, DV], F32, name="result")
-            nc.scalar.activation(result[:], acc[b][:], ACT.Copy, scale=-1.0)
-            nc.sync.dma_start(out[rows(b), :], result[:])
-
-        x_first = [x_gather(0, g) for g in range(PASSES)]
-        factors = dy_gather(0)
+        tw_columns()
         for g in range(PASSES):
-            x_quantise(0, g, x_first[g])
-        pending = None
+            x_gather(0, g)
+        square_late(2, 0)
+        x_weave(0, 0)
+        scale_late(2, 0, 0)
+        x_weave(0, 1)
+        scale_late(2, 0, 1)
+        x_weave(0, 2)
+        square_late(2, 1)
+        x_weave(0, 3)
         for b in range(DY_BLOCKS):
-            following = dy_gather(b + 1) if b + 1 < DY_BLOCKS else None
-            if pending is not None:
-                dz_quantise(b - 1, pending)
-            pending = dz_form(*factors)
-            factors = following
-        x_last = [x_gather(1, g) for g in range(2)]
-        dz_quantise(DY_BLOCKS - 1, pending)
-        for g in range(PASSES):
-            product(0, g)
-        store(0)
-        x_last.extend(x_gather(1, g) for g in range(2, PASSES))
-        for g in range(PASSES):
-            x_quantise(1, g, x_last[g])
-            product(1, g)
-        store(1)
+            dy_gather(b)
+        x_quantise(0, 0, PASSES)
+        scale_late(2, 1, 0)
+        scale_late(2, 1, 1)
+        for j in range(2):
+            square_late(3, j)
+            scale_late(3, j, 0)
+            scale_late(3, j, 1)
+        turn_back(2, 0)
+        square_early(0)
+        turn_back(2, 1)
+        square_early(1)
+        dz_gather(0, 2)
+        dz_form(0)
+        dz_gather(1, 2)
+        dz_form(1)
+        dz_weave(0, 2)
+        turn_back(2, 2)
+        weave_words(0)
+        square_early(2)
+        turn_back(2, 3)
+        dz_gather(2, 2)
+        dz_form(2)
+        dz_gather(3, 2)
+        dz_weave(1, 2)
+        square_early(3)
+        dz_form(3)
+        weave_words(1)
+        dz_weave(2, 2)
+        weave_words(2)
+        x_gather(1, 0)
+        dz_weave(3, 2)
+        x_gather(1, 1)
+        weave_words(3)
+        turn_back(3, 0)
+        turn_back(3, 1)
+        dz_quantise(0, 0, 2)
+        dz_gather(0, 3)
+        dz_gather(1, 3)
+        x_weave(1, 0)
+        turn_back(3, 2)
+        x_weave(1, 1)
+        turn_back(3, 3)
+        x_quantise(1, 0, 2)
+        dz_gather(2, 3)
+        dz_gather(3, 3)
+        for g in range(2):
+            product(acc[0], 0, g)
+        dz_weave(0, 3)
+        for g in range(2):
+            product(acc[1], 1, g)
+        dz_weave(1, 3)
+        x_gather(1, 2)
+        dz_weave(2, 3)
+        x_gather(1, 3)
+        dz_weave(3, 3)
+        x_weave(1, 2)
+        x_weave(1, 3)
+        dz_quantise(1, 0, 2)
+        x_quantise(1, 2, 3)
+        x_quantise(1, 3, 4)
+        for b in range(X_BLOCKS):
+            for g in range(2, PASSES):
+                product(acc[b], b, g)
+        result = [keep.tile([P, DV], F32, name="result%d" % b) for b in range(X_BLOCKS)]
+        nc.scalar.activation(result[0][:], acc[0][:], ACT.Copy, scale=-1.0)
+        nc.sync.dma_start(out[rows(0), :], result[0][:])
+        for j, queue in enumerate((nc.sync, nc.scalar)):
+            cols = slice(j * DV // 2, (j + 1) * DV // 2)
+            nc.vector.tensor_scalar(result[1][:, cols], acc[1][:, cols], -1.0, None, ALU.mult)
+            queue.dma_start(out[rows(1), cols], result[1][:, cols])

@@ -19,13 +19,15 @@ ALU = mybir.AluOpType
 P = 128
 PACK = 4
 K_PASS = P * PACK
+WORDS = K_PASS // 2
 PASSES = E // K_PASS
 LIST_COLS = K_PASS // 16
 X_BLOCKS = D // P
 DY_BLOCKS = DV // P
-HALF = E // 2
+EARLY = PASSES - 1
+LAST = PASSES - 1
 CHUNKS = K_PASS // P
-RING = 5
+RING = 6
 
 
 def tile_attend_gmw_sig_kernel(tc, xT, dyT, hE, sw, tw, offs, offs2, out):
@@ -38,30 +40,32 @@ def tile_attend_gmw_sig_kernel(tc, xT, dyT, hE, sw, tw, offs, offs2, out):
         dst = keep.tile([P, E // 16], U16, name="dst")
         x_tab = [keep.tile([P, V], F32, name="x_tab%d" % b) for b in range(X_BLOCKS)]
         dy_tab = [keep.tile([P, V], F32, name="dy_tab%d" % b) for b in range(DY_BLOCKS)]
-        h_early = [keep.tile([P, HALF], F32, name="h_early%d" % b) for b in range(DY_BLOCKS)]
-        h_late = {(g, j): keep.tile([P, 2, K_PASS], F32, name="h_late%d_%d" % (g, j)) for g in (2, 3) for j in range(2)}
+        h_early = [keep.tile([P, EARLY * K_PASS], F32, name="h_early%d" % b) for b in range(DY_BLOCKS)]
+        h_late = [keep.tile([P, 2, K_PASS], F32, name="h_late%d" % j) for j in range(2)]
         sw_first = [keep.tile([P, K_PASS // 2], F32, name="sw_first%d" % j) for j in range(2)]
         sw_in = {g: keep.tile([P, K_PASS], F32, name="sw_in%d" % g) for g in range(1, PASSES)}
-        tw_in = [keep.tile([P, K_PASS], F32, name="tw_in%d" % g) for g in range(2)]
+        tw_in = [keep.tile([P, K_PASS], F32, name="tw_in%d" % g) for g in range(EARLY)]
         tw_rows = keep.tile([P, P], F32, name="tw_rows")
-        tw_col = keep.tile([P, 8], F32, name="tw_col")
-        tw_bias = keep.tile([P, 8], F32, name="tw_bias")
+        tw_col = keep.tile([P, CHUNKS], F32, name="tw_col")
+        tw_bias = keep.tile([P, CHUNKS], F32, name="tw_bias")
         ident = keep.tile([P, P], F32, name="ident")
-        gathered = [keep.tile([P, K_PASS], F32, name="gathered%d" % i) for i in range(10)]
-        dz_early = [keep.tile([P, HALF], BF16, name="dz_early%d" % b) for b in range(DY_BLOCKS)]
-        banks = [psum.tile([P, PACK, P], F32, name="bank%d" % i) for i in range(RING)]
-        acc = [psum.tile([P, DV], F32, name="acc%d" % b) for b in range(X_BLOCKS)]
-        weighted = [keep.tile([P, HALF], F32, name="weighted%d" % b) for b in range(DY_BLOCKS)]
-        centred = [keep.tile([P, HALF], F32, name="centred%d" % b) for b in range(DY_BLOCKS)]
-        centred_late = {(g, j): keep.tile([P, 2, K_PASS], F32, name="centred_late%d_%d" % (g, j)) for g in (2, 3) for j in range(2)}
-        factor_t = {(g, j, c): keep.tile([P, 2 * P], F32, name="factor_t%d_%d_%d" % (g, j, c)) for g in (2, 3) for j in range(2) for c in range(CHUNKS)}
-        factor = {(g, b): keep.tile([P, K_PASS], F32, name="factor%d_%d" % (g, b)) for g in (2, 3) for b in range(DY_BLOCKS)}
+        gathered = [keep.tile([P, K_PASS], F32, name="gathered%d" % i) for i in range(8)]
+        weighted = [keep.tile([P, EARLY * K_PASS], F32, name="weighted%d" % b) for b in range(2)]
+        centred = [keep.tile([P, EARLY * K_PASS], F32, name="centred%d" % b) for b in range(2)]
+        dz_early = [keep.tile([P, EARLY * K_PASS], BF16, name="dz_early%d" % b) for b in range(DY_BLOCKS)]
+        centred_late = [keep.tile([P, 2, K_PASS], F32, name="centred_late%d" % j) for j in range(2)]
+        factor_t = [keep.tile([P, DV], F32, name="factor_t%d" % c) for c in range(CHUNKS)]
+        factor = [keep.tile([P, K_PASS], F32, name="factor%d" % b) for b in range(DY_BLOCKS)]
+        x_last = keep.tile([P, K_PASS], BF16, name="x_last")
         x_woven = [keep.tile([P, PASSES, K_PASS], BF16, name="x_woven%d" % b, align_bytes=64) for b in range(X_BLOCKS)]
         x_codes = [keep.tile([P, PASSES * P], U32, name="x_codes%d" % b, align_bytes=64) for b in range(X_BLOCKS)]
         x_scales = [keep.tile([P, PASSES * P], U8, name="x_scales%d" % b, align_bytes=64) for b in range(X_BLOCKS)]
+        x_woven_last = keep.tile([P, K_PASS], BF16, name="x_woven_last", align_bytes=64)
         dz_woven = [keep.tile([P, 2, DV * PACK], BF16, name="dz_woven%d" % j, align_bytes=64) for j in range(2)]
         dz_codes = [keep.tile([P, 2 * DV], U32, name="dz_codes%d" % j, align_bytes=64) for j in range(2)]
         dz_scales = [keep.tile([P, 2 * DV], U8, name="dz_scales%d" % j, align_bytes=64) for j in range(2)]
+        banks = [psum.tile([P, PACK, P], F32, name="bank%d" % i) for i in range(RING)]
+        acc = [psum.tile([P, DV], F32, name="acc%d" % b) for b in range(X_BLOCKS)]
 
         def edges(g):
             return slice(g * K_PASS, (g + 1) * K_PASS)
@@ -72,11 +76,11 @@ def tile_attend_gmw_sig_kernel(tc, xT, dyT, hE, sw, tw, offs, offs2, out):
         def rows(b):
             return slice(b * P, (b + 1) * P)
 
-        def load_h_late(g, j):
-            nc.sync.dma_start(h_late[g, j][:], hE[2 * j * P : 2 * (j + 1) * P, edges(g)].rearrange("(b p) e -> p b e", p=P))
+        def load_h_late(j):
+            nc.sync.dma_start(h_late[j][:], hE[2 * j * P : 2 * (j + 1) * P, edges(LAST)].rearrange("(b p) e -> p b e", p=P))
 
         def load_h_early(b):
-            nc.sync.dma_start(h_early[b][:], hE[rows(b), 0:HALF])
+            nc.sync.dma_start(h_early[b][:], hE[rows(b), 0 : EARLY * K_PASS])
 
         def load_dy(b):
             nc.sync.dma_start(dy_tab[b][:], dyT[rows(b), :])
@@ -87,23 +91,20 @@ def tile_attend_gmw_sig_kernel(tc, xT, dyT, hE, sw, tw, offs, offs2, out):
         nc.sync.dma_start(x_tab[0][:], xT[rows(0), :])
         for j in range(2):
             nc.sync.dma_start(sw_first[j][:], sw[:, j * K_PASS // 2 : (j + 1) * K_PASS // 2])
-        nc.sync.dma_start(sw_in[1][:], sw[:, edges(1)])
-        nc.scalar.dma_start(tw_rows[0:8, :], tw[0:1, HALF:E].rearrange("o (c p) -> (o c) p", p=P))
-        load_h_late(2, 0)
-        nc.sync.dma_start(sw_in[2][:], sw[:, edges(2)])
-        nc.sync.dma_start(sw_in[3][:], sw[:, edges(3)])
+        nc.scalar.dma_start(tw_rows[0:CHUNKS, :], tw[0:1, edges(LAST)].rearrange("o (c p) -> (o c) p", p=P))
+        for g in range(1, PASSES):
+            nc.sync.dma_start(sw_in[g][:], sw[:, edges(g)])
         nc.sync.dma_start(dst[:], offs2)
         load_dy(0)
-        nc.sync.dma_start(tw_in[0][:], tw[:, edges(0)])
-        nc.sync.dma_start(tw_in[1][:], tw[:, edges(1)])
+        for g in range(EARLY):
+            nc.sync.dma_start(tw_in[g][:], tw[:, edges(g)])
+        load_h_late(0)
         load_dy(1)
-        load_h_late(2, 1)
-        load_h_late(3, 0)
-        load_dy(2)
-        load_h_late(3, 1)
         load_h_early(0)
-        load_dy(3)
+        load_h_late(1)
+        load_dy(2)
         load_h_early(1)
+        load_dy(3)
         load_h_early(2)
         load_h_early(3)
         nc.sync.dma_start(x_tab[1][:], xT[rows(1), :])
@@ -128,20 +129,31 @@ def tile_attend_gmw_sig_kernel(tc, xT, dyT, hE, sw, tw, offs, offs2, out):
                 nc.tensor.transpose(bank[:, t, :], unit[:, t:K_PASS:PACK], ident[:])
             nc.scalar.copy(target.rearrange("p (c t) -> p c t", t=PACK), bank[:].rearrange("p t c -> p c t"))
 
-        x_buf = {(0, 0): 0, (0, 1): 1, (0, 2): 2, (0, 3): 3, (1, 0): 2, (1, 1): 3, (1, 2): 1, (1, 3): 2}
-        dz_buf = {(0, 2): 0, (1, 2): 1, (2, 2): 2, (3, 2): 3, (0, 3): 0, (1, 3): 1, (2, 3): 2, (3, 3): 3}
-
         def x_gather(b, g):
-            gather(gathered[x_buf[b, g]], x_tab[b], src, g, sw_first if g == 0 else [sw_in[g]])
+            gather(gathered[g], x_tab[b], src, g, sw_first if g == 0 else [sw_in[g]])
 
         def x_weave(b, g):
-            weave(gathered[x_buf[b, g]], x_woven[b][:, g, :])
+            weave(gathered[g], x_woven[b][:, g, :])
 
-        def dz_gather(b, g):
-            gather(gathered[dz_buf[b, g]], dy_tab[b], dst, g, [factor[g, b]])
+        def x_weave_last():
+            nc.vector.tensor_copy(
+                x_last[:].rearrange("p (u s j) -> p u s j", u=2, j=2),
+                gathered[LAST][:].rearrange("p (s u j) -> p u s j", u=2, j=2),
+            )
+            words = x_last[:].bitcast(F32)
+            bank = next_bank()
+            for u in range(2):
+                nc.tensor.transpose(bank[:, u, :], words[:, rows(u)], ident[:])
+            nc.scalar.copy(
+                x_woven_last[:].bitcast(F32).rearrange("p (n u) -> p n u", u=2),
+                bank[:, 0:2, :].rearrange("p u n -> p n u"),
+            )
 
-        def dz_weave(b, g):
-            weave(gathered[dz_buf[b, g]], dz_woven[1][:, g - 2, b * K_PASS : (b + 1) * K_PASS])
+        def dz_gather(b):
+            gather(gathered[PASSES + b], dy_tab[b], dst, LAST, [factor[b]])
+
+        def dz_weave(b):
+            weave(gathered[PASSES + b], dz_woven[1][:, 1, b * K_PASS : (b + 1) * K_PASS])
 
         def x_quantise(b, first, last):
             nc.vector.quantize_mx(
@@ -149,6 +161,9 @@ def tile_attend_gmw_sig_kernel(tc, xT, dyT, hE, sw, tw, offs, offs2, out):
                 scales=x_scales[b][:, first * P : last * P],
                 in_=x_woven[b][:, first:last, :].rearrange("p g c -> p (g c)"),
             )
+
+        def x_quantise_last():
+            nc.vector.quantize_mx(out=x_codes[1][:, rows(LAST)].bitcast(E4M3), scales=x_scales[1][:, rows(LAST)], in_=x_woven_last[:])
 
         def dz_quantise(j, first, last):
             nc.vector.quantize_mx(
@@ -160,58 +175,65 @@ def tile_attend_gmw_sig_kernel(tc, xT, dyT, hE, sw, tw, offs, offs2, out):
         def tw_columns():
             bank = next_bank()
             nc.tensor.transpose(bank[:, 0, :], tw_rows[:], ident[:])
-            nc.scalar.copy(tw_col[:], bank[:, 0, 0:8])
-            nc.scalar.activation(tw_bias[:], bank[:, 0, 0:8], ACT.Copy, scale=-0.25)
+            nc.scalar.copy(tw_col[:], bank[:, 0, 0:CHUNKS])
+            nc.scalar.activation(tw_bias[:], bank[:, 0, 0:CHUNKS], ACT.Copy, scale=-0.25)
 
-        def square_late(g, j):
-            nc.scalar.activation(centred_late[g, j][:], h_late[g, j][:], ACT.Square, bias=-0.5, scale=1.0)
+        def square_late(j):
+            nc.scalar.activation(centred_late[j][:], h_late[j][:], ACT.Square, bias=-0.5, scale=1.0)
 
-        def scale_late(g, j, half):
+        def scale_late(c):
             bank = next_bank()
-            for i in range(2):
-                for b in range(2):
-                    nc.tensor.transpose(bank[:, 2 * i + b, :], centred_late[g, j][:, b, rows(2 * half + i)], ident[:])
-            for i in range(2):
-                c = 2 * half + i
-                col = (g - 2) * CHUNKS + c
-                nc.scalar.activation(
-                    factor_t[g, j, c][:],
-                    bank[:, 2 * i : 2 * i + 2, :].rearrange("p b n -> p (b n)"),
-                    ACT.Identity,
-                    bias=tw_bias[:, col : col + 1],
-                    scale=tw_col[:, col : col + 1],
-                )
+            for b in range(DY_BLOCKS):
+                nc.tensor.transpose(bank[:, b, :], centred_late[b // 2][:, b % 2, rows(c)], ident[:])
+            nc.scalar.activation(
+                factor_t[c][:],
+                bank[:].rearrange("p b n -> p (b n)"),
+                ACT.Identity,
+                bias=tw_bias[:, c : c + 1],
+                scale=tw_col[:, c : c + 1],
+            )
 
-        def turn_back(g, b):
+        def turn_back(b):
             bank = next_bank()
             for c in range(CHUNKS):
-                nc.tensor.transpose(bank[:, c, :], factor_t[g, b // 2, c][:, rows(b % 2)], ident[:])
-            nc.scalar.copy(factor[g, b][:], bank[:].rearrange("p c e -> p (c e)"))
+                nc.tensor.transpose(bank[:, c, :], factor_t[c][:, rows(b)], ident[:])
+            nc.scalar.copy(factor[b][:], bank[:].rearrange("p c e -> p (c e)"))
 
-        def dy_gather(b):
-            for g in range(2):
-                nc.vector.tensor_tensor(weighted[b][:, edges(g)], dy_tab[b][:].indirect(dst[:, entries(g)]), tw_in[g][:], ALU.mult)
+        def dy_gather(b, g):
+            nc.vector.tensor_tensor(weighted[b % 2][:, edges(g)], dy_tab[b][:].indirect(dst[:, entries(g)]), tw_in[g][:], ALU.mult)
 
         def square_early(b):
-            nc.scalar.activation(centred[b][:], h_early[b][:], ACT.Square, bias=-0.5, scale=1.0)
+            nc.scalar.activation(centred[b % 2][:], h_early[b][:], ACT.Square, bias=-0.5, scale=1.0)
 
         def dz_form(b):
-            nc.vector.scalar_tensor_tensor(dz_early[b][:], centred[b][:], 0.25, weighted[b][:], ALU.subtract, ALU.mult)
+            nc.vector.scalar_tensor_tensor(dz_early[b][:], centred[b % 2][:], 0.25, weighted[b % 2][:], ALU.subtract, ALU.mult)
+
+        def turn_words(bank, place, b, g):
+            words = dz_early[b][:].bitcast(F32)
+            for u in range(2):
+                nc.tensor.transpose(bank[:, 2 * place + u, :], words[:, WORDS * g + u : WORDS * (g + 1) : 2], ident[:])
 
         def weave_words(b):
-            words = dz_early[b][:].bitcast(F32)
             bank = next_bank()
             for g in range(2):
-                for u in range(2):
-                    nc.tensor.transpose(bank[:, 2 * g + u, :], words[:, 256 * g + u : 256 * (g + 1) : 2], ident[:])
+                turn_words(bank, g, b, g)
             nc.scalar.copy(
                 dz_woven[0][:, :, b * K_PASS : (b + 1) * K_PASS].bitcast(F32).rearrange("p g (n u) -> p g n u", u=2),
                 bank[:].rearrange("p (g u) n -> p g n u", u=2),
             )
 
-        def product(acc, b, g):
+        def weave_words_third(j):
+            bank = next_bank()
+            for i in range(2):
+                turn_words(bank, i, 2 * j + i, 2)
+            nc.scalar.copy(
+                dz_woven[1][:, 0, 2 * j * K_PASS : 2 * (j + 1) * K_PASS].bitcast(F32).rearrange("p (i n u) -> p i n u", i=2, u=2),
+                bank[:].rearrange("p (i u) n -> p i n u", u=2),
+            )
+
+        def product(b, g):
             nc.tensor.matmul_mx(
-                out=acc[:],
+                out=acc[b][:],
                 lhsT=x_codes[b][:, g * P : (g + 1) * P].bitcast(E4M3),
                 lhsT_scale=x_scales[b][:, g * P : (g + 1) * P],
                 rhs=dz_codes[g // 2][:, (g % 2) * DV : (g % 2 + 1) * DV].bitcast(E5M2),
@@ -223,79 +245,68 @@ def tile_attend_gmw_sig_kernel(tc, xT, dyT, hE, sw, tw, offs, offs2, out):
         tw_columns()
         for g in range(PASSES):
             x_gather(0, g)
-        square_late(2, 0)
-        x_weave(0, 0)
-        scale_late(2, 0, 0)
-        x_weave(0, 1)
-        scale_late(2, 0, 1)
-        x_weave(0, 2)
-        square_late(2, 1)
-        x_weave(0, 3)
-        for b in range(DY_BLOCKS):
-            dy_gather(b)
+            x_weave(0, g)
+        for g in range(EARLY):
+            dy_gather(0, g)
+        square_late(0)
+        for g in range(EARLY):
+            dy_gather(1, g)
         x_quantise(0, 0, PASSES)
-        scale_late(2, 1, 0)
-        scale_late(2, 1, 1)
-        for j in range(2):
-            square_late(3, j)
-            scale_late(3, j, 0)
-            scale_late(3, j, 1)
-        turn_back(2, 0)
         square_early(0)
-        turn_back(2, 1)
-        square_early(1)
-        dz_gather(0, 2)
+        square_late(1)
         dz_form(0)
-        dz_gather(1, 2)
+        for c in range(CHUNKS):
+            scale_late(c)
+        dy_gather(2, 0)
+        square_early(1)
         dz_form(1)
-        dz_weave(0, 2)
-        turn_back(2, 2)
-        weave_words(0)
+        dy_gather(2, 1)
+        dy_gather(2, 2)
         square_early(2)
-        turn_back(2, 3)
-        dz_gather(2, 2)
+        for b in range(DY_BLOCKS):
+            turn_back(b)
+        weave_words(0)
+        dz_gather(0)
         dz_form(2)
-        dz_gather(3, 2)
-        dz_weave(1, 2)
+        dy_gather(3, 0)
         square_early(3)
-        dz_form(3)
         weave_words(1)
-        dz_weave(2, 2)
+        weave_words_third(0)
+        dz_weave(0)
+        dz_gather(1)
+        dy_gather(3, 1)
+        dy_gather(3, 2)
         weave_words(2)
-        x_gather(1, 0)
-        dz_weave(3, 2)
-        x_gather(1, 1)
+        dz_weave(1)
+        dz_gather(2)
+        dz_form(3)
+        dz_gather(3)
+        dz_weave(2)
         weave_words(3)
-        turn_back(3, 0)
-        turn_back(3, 1)
+        weave_words_third(1)
+        x_gather(1, 0)
+        dz_weave(3)
         dz_quantise(0, 0, 2)
-        dz_gather(0, 3)
-        dz_gather(1, 3)
+        x_gather(1, 1)
         x_weave(1, 0)
-        turn_back(3, 2)
-        x_weave(1, 1)
-        turn_back(3, 3)
-        x_quantise(1, 0, 2)
-        dz_gather(2, 3)
-        dz_gather(3, 3)
+        dz_quantise(1, 0, 1)
         for g in range(2):
-            product(acc[0], 0, g)
-        dz_weave(0, 3)
-        for g in range(2):
-            product(acc[1], 1, g)
-        dz_weave(1, 3)
+            product(0, g)
         x_gather(1, 2)
-        dz_weave(2, 3)
-        x_gather(1, 3)
-        dz_weave(3, 3)
+        x_weave(1, 1)
+        product(0, 2)
         x_weave(1, 2)
-        x_weave(1, 3)
-        dz_quantise(1, 0, 2)
+        x_quantise(1, 0, 2)
+        x_gather(1, 3)
+        for g in range(2):
+            product(1, g)
+        x_weave_last()
+        dz_quantise(1, 1, 2)
         x_quantise(1, 2, 3)
-        x_quantise(1, 3, 4)
-        for b in range(X_BLOCKS):
-            for g in range(2, PASSES):
-                product(acc[b], b, g)
+        x_quantise_last()
+        product(0, 3)
+        for g in range(2, PASSES):
+            product(1, g)
         result = [keep.tile([P, DV], F32, name="result%d" % b) for b in range(X_BLOCKS)]
         nc.scalar.activation(result[0][:], acc[0][:], ACT.Copy, scale=-1.0)
         nc.sync.dma_start(out[rows(0), :], result[0][:])

@@ -19,15 +19,15 @@ ALU = mybir.AluOpType
 P = 128
 PACK = 4
 K_PASS = P * PACK
-WORDS = K_PASS // 2
 PASSES = E // K_PASS
-LIST_COLS = K_PASS // 16
+PAIRS = K_PASS // 2
+LIST_ROWS = 16
 X_BLOCKS = D // P
 DY_BLOCKS = DV // P
 EARLY = PASSES - 1
 LAST = PASSES - 1
 CHUNKS = K_PASS // P
-RING = 6
+TURN_BANKS = 8 - X_BLOCKS
 
 
 def tile_attend_gmw_sig_kernel(tc, xT, dyT, hE, sw, tw, offs, offs2, out):
@@ -36,61 +36,66 @@ def tile_attend_gmw_sig_kernel(tc, xT, dyT, hE, sw, tw, offs, offs2, out):
         keep = ctx.enter_context(tc.tile_pool(name="keep", bufs=1))
         psum = ctx.enter_context(tc.psum_pool(name="psum", bufs=1))
 
-        src = keep.tile([P, E // 16], U16, name="src")
-        dst = keep.tile([P, E // 16], U16, name="dst")
+        src = keep.tile([P, E // LIST_ROWS], U16, name="src")
+        dst = keep.tile([P, E // LIST_ROWS], U16, name="dst")
         x_tab = [keep.tile([P, V], F32, name="x_tab%d" % b) for b in range(X_BLOCKS)]
         dy_tab = [keep.tile([P, V], F32, name="dy_tab%d" % b) for b in range(DY_BLOCKS)]
         h_early = [keep.tile([P, EARLY * K_PASS], F32, name="h_early%d" % b) for b in range(DY_BLOCKS)]
-        h_late = [keep.tile([P, 2, K_PASS], F32, name="h_late%d" % j) for j in range(2)]
-        sw_first = [keep.tile([P, K_PASS // 2], F32, name="sw_first%d" % j) for j in range(2)]
-        sw_in = {g: keep.tile([P, K_PASS], F32, name="sw_in%d" % g) for g in range(1, PASSES)}
+        h_last = [keep.tile([P, 2, K_PASS], F32, name="h_last%d" % j) for j in range(2)]
+        sw_in = [keep.tile([P, K_PASS], F32, name="sw_in%d" % g) for g in range(PASSES)]
         tw_in = [keep.tile([P, K_PASS], F32, name="tw_in%d" % g) for g in range(EARLY)]
         tw_rows = keep.tile([P, P], F32, name="tw_rows")
         tw_col = keep.tile([P, CHUNKS], F32, name="tw_col")
         tw_bias = keep.tile([P, CHUNKS], F32, name="tw_bias")
         ident = keep.tile([P, P], F32, name="ident")
-        gathered = [keep.tile([P, K_PASS], F32, name="gathered%d" % i) for i in range(8)]
-        weighted = [keep.tile([P, EARLY * K_PASS], F32, name="weighted%d" % b) for b in range(2)]
-        centred = [keep.tile([P, EARLY * K_PASS], F32, name="centred%d" % b) for b in range(2)]
+        xe_first = [keep.tile([P, K_PASS], F32, name="xe_first%d" % g) for g in range(PASSES)]
+        weighted = [keep.tile([P, EARLY * K_PASS], F32, name="weighted%d" % b) for b in range(DY_BLOCKS)]
+        dz_last = [keep.tile([P, K_PASS], F32, name="dz_last%d" % b) for b in range(DY_BLOCKS)]
+        square_early = [keep.tile([P, EARLY * K_PASS], F32, name="square_early%d" % b) for b in range(DY_BLOCKS)]
         dz_early = [keep.tile([P, EARLY * K_PASS], BF16, name="dz_early%d" % b) for b in range(DY_BLOCKS)]
-        centred_late = [keep.tile([P, 2, K_PASS], F32, name="centred_late%d" % j) for j in range(2)]
-        factor_t = [keep.tile([P, DV], F32, name="factor_t%d" % c) for c in range(CHUNKS)]
+        square_last = [keep.tile([P, 2, K_PASS], F32, name="square_last%d" % j) for j in range(2)]
+        factor_turned = [keep.tile([P, DV], F32, name="factor_turned%d" % c) for c in range(CHUNKS)]
         factor = [keep.tile([P, K_PASS], F32, name="factor%d" % b) for b in range(DY_BLOCKS)]
-        x_last = keep.tile([P, K_PASS], BF16, name="x_last")
-        x_woven = [keep.tile([P, PASSES, K_PASS], BF16, name="x_woven%d" % b, align_bytes=64) for b in range(X_BLOCKS)]
+        result = [keep.tile([P, DV], F32, name="result%d" % b) for b in range(X_BLOCKS)]
+        x_woven = [keep.tile([P, PASSES - b, K_PASS], BF16, name="x_woven%d" % b, align_bytes=64) for b in range(X_BLOCKS)]
         x_codes = [keep.tile([P, PASSES * P], U32, name="x_codes%d" % b, align_bytes=64) for b in range(X_BLOCKS)]
         x_scales = [keep.tile([P, PASSES * P], U8, name="x_scales%d" % b, align_bytes=64) for b in range(X_BLOCKS)]
-        x_woven_last = keep.tile([P, K_PASS], BF16, name="x_woven_last", align_bytes=64)
+        x_end_woven = keep.tile([P, K_PASS], BF16, name="x_end_woven", align_bytes=64)
         dz_woven = [keep.tile([P, 2, DV * PACK], BF16, name="dz_woven%d" % j, align_bytes=64) for j in range(2)]
         dz_codes = [keep.tile([P, 2 * DV], U32, name="dz_codes%d" % j, align_bytes=64) for j in range(2)]
         dz_scales = [keep.tile([P, 2 * DV], U8, name="dz_scales%d" % j, align_bytes=64) for j in range(2)]
-        banks = [psum.tile([P, PACK, P], F32, name="bank%d" % i) for i in range(RING)]
-        acc = [psum.tile([P, DV], F32, name="acc%d" % b) for b in range(X_BLOCKS)]
+        banks = [psum.tile([P, PACK, P], F32, name="bank%d" % i) for i in range(TURN_BANKS)]
+        sums = [psum.tile([P, DV], F32, name="sums%d" % b) for b in range(X_BLOCKS)]
 
         def edges(g):
             return slice(g * K_PASS, (g + 1) * K_PASS)
 
-        def entries(g):
-            return slice(g * LIST_COLS, (g + 1) * LIST_COLS)
+        def half(j):
+            return slice(j * K_PASS // 2, (j + 1) * K_PASS // 2)
 
-        def rows(b):
-            return slice(b * P, (b + 1) * P)
+        def run(i):
+            return slice(i * P, (i + 1) * P)
 
-        def load_h_late(j):
-            nc.sync.dma_start(h_late[j][:], hE[2 * j * P : 2 * (j + 1) * P, edges(LAST)].rearrange("(b p) e -> p b e", p=P))
+        xe = {(0, g): xe_first[g][:] for g in range(PASSES)}
+        for j in range(2):
+            xe[1, j] = weighted[DY_BLOCKS - 1][:, edges(j)]
+            xe[1, 2 + j] = dz_woven[j][:, 0, 0 : 2 * K_PASS].bitcast(F32)
+
+        def load_h_last(j):
+            nc.sync.dma_start(h_last[j][:], hE[2 * j * P : 2 * (j + 1) * P, edges(LAST)].rearrange("(b p) e -> p b e", p=P))
 
         def load_h_early(b):
-            nc.sync.dma_start(h_early[b][:], hE[rows(b), 0 : EARLY * K_PASS])
+            nc.sync.dma_start(h_early[b][:], hE[run(b), 0 : EARLY * K_PASS])
 
         def load_dy(b):
-            nc.sync.dma_start(dy_tab[b][:], dyT[rows(b), :])
+            nc.sync.dma_start(dy_tab[b][:], dyT[run(b), :])
 
         nc.gpsimd.memset(tw_rows[:], 0.0)
         make_identity(nc, ident[:])
         nc.sync.dma_start(src[:], offs)
-        nc.sync.dma_start(x_tab[0][:], xT[rows(0), :])
+        nc.sync.dma_start(x_tab[0][:], xT[run(0), :])
         for j in range(2):
-            nc.sync.dma_start(sw_first[j][:], sw[:, j * K_PASS // 2 : (j + 1) * K_PASS // 2])
+            nc.sync.dma_start(sw_in[0][:, half(j)], sw[:, half(j)])
         nc.scalar.dma_start(tw_rows[0:CHUNKS, :], tw[0:1, edges(LAST)].rearrange("o (c p) -> (o c) p", p=P))
         for g in range(1, PASSES):
             nc.sync.dma_start(sw_in[g][:], sw[:, edges(g)])
@@ -98,78 +103,68 @@ def tile_attend_gmw_sig_kernel(tc, xT, dyT, hE, sw, tw, offs, offs2, out):
         load_dy(0)
         for g in range(EARLY):
             nc.sync.dma_start(tw_in[g][:], tw[:, edges(g)])
-        load_h_late(0)
-        load_dy(1)
+        for j in range(2):
+            load_h_last(j)
+            load_dy(1 + j)
         load_h_early(0)
-        load_h_late(1)
-        load_dy(2)
-        load_h_early(1)
-        load_dy(3)
-        load_h_early(2)
-        load_h_early(3)
-        nc.sync.dma_start(x_tab[1][:], xT[rows(1), :])
+        load_dy(DY_BLOCKS - 1)
+        for b in range(1, DY_BLOCKS):
+            load_h_early(b)
+        nc.sync.dma_start(x_tab[1][:], xT[run(1), :])
 
-        used = []
+        taken = []
 
         def next_bank():
-            used.append(None)
-            return banks[(len(used) - 1) % RING]
+            taken.append(len(taken) % TURN_BANKS)
+            return banks[taken[-1]]
 
-        def gather(unit, table, offsets, g, scales):
-            width = K_PASS // len(scales)
-            for j, scale in enumerate(scales):
-                first = g * LIST_COLS + j * width // 16
-                nc.vector.tensor_tensor(
-                    unit[:, j * width : (j + 1) * width], table[:].indirect(offsets[:, first : first + width // 16]), scale[:], ALU.mult
-                )
+        def gather(target, table, offsets, first_edge, scale):
+            columns = slice(first_edge // LIST_ROWS, (first_edge + target.shape[1]) // LIST_ROWS)
+            nc.vector.tensor_tensor(target, table[:].indirect(offsets[:, columns]), scale, ALU.mult)
 
-        def weave(unit, target):
+        def weave(values, target):
             bank = next_bank()
             for t in range(PACK):
-                nc.tensor.transpose(bank[:, t, :], unit[:, t:K_PASS:PACK], ident[:])
+                nc.tensor.transpose(bank[:, t, :], values[:, t:K_PASS:PACK], ident[:])
             nc.scalar.copy(target.rearrange("p (c t) -> p c t", t=PACK), bank[:].rearrange("p t c -> p c t"))
 
         def x_gather(b, g):
-            gather(gathered[g], x_tab[b], src, g, sw_first if g == 0 else [sw_in[g]])
+            gather(xe[b, g], x_tab[b], src, g * K_PASS, sw_in[g][:])
 
         def x_weave(b, g):
-            weave(gathered[g], x_woven[b][:, g, :])
+            weave(xe[b, g], x_woven[b][:, g, :])
 
-        def x_weave_last():
+        def x_weave_end():
+            words = result[0][:, 0:PAIRS]
             nc.vector.tensor_copy(
-                x_last[:].rearrange("p (u s j) -> p u s j", u=2, j=2),
-                gathered[LAST][:].rearrange("p (s u j) -> p u s j", u=2, j=2),
+                words.bitcast(BF16).rearrange("p (u s j) -> p u s j", u=2, j=2),
+                xe[1, LAST].rearrange("p (s u j) -> p u s j", u=2, j=2),
             )
-            words = x_last[:].bitcast(F32)
             bank = next_bank()
             for u in range(2):
-                nc.tensor.transpose(bank[:, u, :], words[:, rows(u)], ident[:])
+                nc.tensor.transpose(bank[:, u, :], words[:, run(u)], ident[:])
             nc.scalar.copy(
-                x_woven_last[:].bitcast(F32).rearrange("p (n u) -> p n u", u=2),
+                x_end_woven[:].bitcast(F32).rearrange("p (n u) -> p n u", u=2),
                 bank[:, 0:2, :].rearrange("p u n -> p n u"),
             )
 
-        def dz_gather(b):
-            gather(gathered[PASSES + b], dy_tab[b], dst, LAST, [factor[b]])
-
-        def dz_weave(b):
-            weave(gathered[PASSES + b], dz_woven[1][:, 1, b * K_PASS : (b + 1) * K_PASS])
-
-        def x_quantise(b, first, last):
+        def x_quantise(b, first, end):
             nc.vector.quantize_mx(
-                out=x_codes[b][:, first * P : last * P].bitcast(E4M3),
-                scales=x_scales[b][:, first * P : last * P],
-                in_=x_woven[b][:, first:last, :].rearrange("p g c -> p (g c)"),
+                out=x_codes[b][:, first * P : end * P].bitcast(E4M3),
+                scales=x_scales[b][:, first * P : end * P],
+                in_=x_woven[b][:, first:end, :].rearrange("p g c -> p (g c)"),
             )
 
-        def x_quantise_last():
-            nc.vector.quantize_mx(out=x_codes[1][:, rows(LAST)].bitcast(E4M3), scales=x_scales[1][:, rows(LAST)], in_=x_woven_last[:])
+        def x_quantise_end():
+            nc.vector.quantize_mx(out=x_codes[1][:, run(LAST)].bitcast(E4M3), scales=x_scales[1][:, run(LAST)], in_=x_end_woven[:])
 
-        def dz_quantise(j, first, last):
+        def dz_quantise(first, end):
+            j, i = divmod(first, 2)
+            count = end - first
             nc.vector.quantize_mx(
-                out=dz_codes[j][:, first * DV : last * DV].bitcast(E5M2),
-                scales=dz_scales[j][:, first * DV : last * DV],
-                in_=dz_woven[j][:, first:last, :].rearrange("p g c -> p (g c)"),
+                out=dz_codes[j][:, i * DV : (i + count) * DV].bitcast(E5M2),
+                scales=dz_scales[j][:, i * DV : (i + count) * DV],
+                in_=dz_woven[j][:, i : i + count, :].rearrange("p g c -> p (g c)"),
             )
 
         def tw_columns():
@@ -178,139 +173,130 @@ def tile_attend_gmw_sig_kernel(tc, xT, dyT, hE, sw, tw, offs, offs2, out):
             nc.scalar.copy(tw_col[:], bank[:, 0, 0:CHUNKS])
             nc.scalar.activation(tw_bias[:], bank[:, 0, 0:CHUNKS], ACT.Copy, scale=-0.25)
 
-        def square_late(j):
-            nc.scalar.activation(centred_late[j][:], h_late[j][:], ACT.Square, bias=-0.5, scale=1.0)
+        def square(target, h):
+            nc.scalar.activation(target[:], h[:], ACT.Square, bias=-0.5, scale=1.0)
 
-        def scale_late(c):
+        def factor_scale(c):
             bank = next_bank()
             for b in range(DY_BLOCKS):
-                nc.tensor.transpose(bank[:, b, :], centred_late[b // 2][:, b % 2, rows(c)], ident[:])
+                nc.tensor.transpose(bank[:, b, :], square_last[b // 2][:, b % 2, run(c)], ident[:])
             nc.scalar.activation(
-                factor_t[c][:],
+                factor_turned[c][:],
                 bank[:].rearrange("p b n -> p (b n)"),
                 ACT.Identity,
                 bias=tw_bias[:, c : c + 1],
                 scale=tw_col[:, c : c + 1],
             )
 
-        def turn_back(b):
+        def factor_turn_back(b):
             bank = next_bank()
             for c in range(CHUNKS):
-                nc.tensor.transpose(bank[:, c, :], factor_t[c][:, rows(b)], ident[:])
+                nc.tensor.transpose(bank[:, c, :], factor_turned[c][:, run(b)], ident[:])
             nc.scalar.copy(factor[b][:], bank[:].rearrange("p c e -> p (c e)"))
 
-        def dy_gather(b, g):
-            nc.vector.tensor_tensor(weighted[b % 2][:, edges(g)], dy_tab[b][:].indirect(dst[:, entries(g)]), tw_in[g][:], ALU.mult)
+        def last_gather(b):
+            gather(dz_last[b][:], dy_tab[b], dst, LAST * K_PASS, factor[b][:])
 
-        def square_early(b):
-            nc.scalar.activation(centred[b % 2][:], h_early[b][:], ACT.Square, bias=-0.5, scale=1.0)
+        def last_weave(b):
+            weave(dz_last[b], dz_woven[LAST // 2][:, LAST % 2, b * K_PASS : (b + 1) * K_PASS])
 
-        def dz_form(b):
-            nc.vector.scalar_tensor_tensor(dz_early[b][:], centred[b % 2][:], 0.25, weighted[b % 2][:], ALU.subtract, ALU.mult)
+        def early_gather(b, g):
+            gather(weighted[b][:, edges(g)], dy_tab[b], dst, g * K_PASS, tw_in[g][:])
 
-        def turn_words(bank, place, b, g):
+        def early_form(b):
+            nc.vector.scalar_tensor_tensor(dz_early[b][:], square_early[b][:], 0.25, weighted[b][:], ALU.subtract, ALU.mult)
+
+        def turn_pairs(bank, place, b, g):
             words = dz_early[b][:].bitcast(F32)
             for u in range(2):
-                nc.tensor.transpose(bank[:, 2 * place + u, :], words[:, WORDS * g + u : WORDS * (g + 1) : 2], ident[:])
+                nc.tensor.transpose(bank[:, 2 * place + u, :], words[:, PAIRS * g + u : PAIRS * (g + 1) : 2], ident[:])
 
-        def weave_words(b):
+        def early_weave_01(b):
             bank = next_bank()
             for g in range(2):
-                turn_words(bank, g, b, g)
+                turn_pairs(bank, g, b, g)
             nc.scalar.copy(
                 dz_woven[0][:, :, b * K_PASS : (b + 1) * K_PASS].bitcast(F32).rearrange("p g (n u) -> p g n u", u=2),
                 bank[:].rearrange("p (g u) n -> p g n u", u=2),
             )
 
-        def weave_words_third(j):
+        def early_weave_2(j):
             bank = next_bank()
             for i in range(2):
-                turn_words(bank, i, 2 * j + i, 2)
+                turn_pairs(bank, i, 2 * j + i, 2)
             nc.scalar.copy(
                 dz_woven[1][:, 0, 2 * j * K_PASS : 2 * (j + 1) * K_PASS].bitcast(F32).rearrange("p (i n u) -> p i n u", i=2, u=2),
                 bank[:].rearrange("p (i u) n -> p i n u", u=2),
             )
 
         def product(b, g):
+            j, i = divmod(g, 2)
             nc.tensor.matmul_mx(
-                out=acc[b][:],
-                lhsT=x_codes[b][:, g * P : (g + 1) * P].bitcast(E4M3),
-                lhsT_scale=x_scales[b][:, g * P : (g + 1) * P],
-                rhs=dz_codes[g // 2][:, (g % 2) * DV : (g % 2 + 1) * DV].bitcast(E5M2),
-                rhs_scale=dz_scales[g // 2][:, (g % 2) * DV : (g % 2 + 1) * DV],
+                out=sums[b][:],
+                lhsT=x_codes[b][:, run(g)].bitcast(E4M3),
+                lhsT_scale=x_scales[b][:, run(g)],
+                rhs=dz_codes[j][:, i * DV : (i + 1) * DV].bitcast(E5M2),
+                rhs_scale=dz_scales[j][:, i * DV : (i + 1) * DV],
                 start=(g == 0),
-                stop=(g == PASSES - 1),
+                stop=(g == LAST),
             )
 
         tw_columns()
-        for g in range(PASSES):
+        for j in range(2):
+            gather(xe[0, 0][:, half(j)], x_tab[0], src, half(j).start, sw_in[0][:, half(j)])
+        for g in range(1, PASSES):
             x_gather(0, g)
+        for g in range(LAST):
             x_weave(0, g)
-        for g in range(EARLY):
-            dy_gather(0, g)
-        square_late(0)
-        for g in range(EARLY):
-            dy_gather(1, g)
-        x_quantise(0, 0, PASSES)
-        square_early(0)
-        square_late(1)
-        dz_form(0)
-        for c in range(CHUNKS):
-            scale_late(c)
-        dy_gather(2, 0)
-        square_early(1)
-        dz_form(1)
-        dy_gather(2, 1)
-        dy_gather(2, 2)
-        square_early(2)
         for b in range(DY_BLOCKS):
-            turn_back(b)
-        weave_words(0)
-        dz_gather(0)
-        dz_form(2)
-        dy_gather(3, 0)
-        square_early(3)
-        weave_words(1)
-        weave_words_third(0)
-        dz_weave(0)
-        dz_gather(1)
-        dy_gather(3, 1)
-        dy_gather(3, 2)
-        weave_words(2)
-        dz_weave(1)
-        dz_gather(2)
-        dz_form(3)
-        dz_gather(3)
-        dz_weave(2)
-        weave_words(3)
-        weave_words_third(1)
+            for g in range(EARLY):
+                early_gather(b, g)
+        for j in range(2):
+            square(square_last[j], h_last[j])
+        for c in range(CHUNKS):
+            factor_scale(c)
+        square(square_early[0], h_early[0])
+        for b in range(2):
+            factor_turn_back(b)
+        x_weave(0, LAST)
+        for b in range(2, DY_BLOCKS):
+            factor_turn_back(b)
+        for b in range(1, DY_BLOCKS):
+            square(square_early[b], h_early[b])
+        x_quantise(0, 0, PASSES)
+        for b in range(DY_BLOCKS):
+            last_gather(b)
+            early_form(b)
+        for b in range(DY_BLOCKS):
+            last_weave(b)
+            early_weave_01(b)
+            if b % 2:
+                early_weave_2(b // 2)
         x_gather(1, 0)
-        dz_weave(3)
-        dz_quantise(0, 0, 2)
         x_gather(1, 1)
         x_weave(1, 0)
-        dz_quantise(1, 0, 1)
-        for g in range(2):
-            product(0, g)
-        x_gather(1, 2)
+        dz_quantise(0, 2)
+        dz_quantise(2, 3)
         x_weave(1, 1)
-        product(0, 2)
-        x_weave(1, 2)
+        x_gather(1, 2)
+        for g in range(EARLY):
+            product(0, g)
         x_quantise(1, 0, 2)
-        x_gather(1, 3)
+        x_weave(1, 2)
+        x_gather(1, LAST)
         for g in range(2):
             product(1, g)
-        x_weave_last()
-        dz_quantise(1, 1, 2)
-        x_quantise(1, 2, 3)
-        x_quantise_last()
-        product(0, 3)
-        for g in range(2, PASSES):
-            product(1, g)
-        result = [keep.tile([P, DV], F32, name="result%d" % b) for b in range(X_BLOCKS)]
-        nc.scalar.activation(result[0][:], acc[0][:], ACT.Copy, scale=-1.0)
-        nc.sync.dma_start(out[rows(0), :], result[0][:])
+        x_weave_end()
+        dz_quantise(LAST, PASSES)
+        x_quantise(1, 2, LAST)
+        product(0, LAST)
+        product(1, 2)
+        x_quantise_end()
+        product(1, LAST)
+
+        nc.scalar.activation(result[0][:], sums[0][:], ACT.Copy, scale=-1.0)
+        nc.sync.dma_start(out[run(0), :], result[0][:])
         for j, queue in enumerate((nc.sync, nc.scalar)):
             cols = slice(j * DV // 2, (j + 1) * DV // 2)
-            nc.vector.tensor_scalar(result[1][:, cols], acc[1][:, cols], -1.0, None, ALU.mult)
-            queue.dma_start(out[rows(1), cols], result[1][:, cols])
+            nc.vector.tensor_scalar(result[1][:, cols], sums[1][:, cols], -1.0, None, ALU.mult)
+            queue.dma_start(out[run(1), cols], result[1][:, cols])

@@ -24,8 +24,10 @@ PAIRS = K_PASS // 2
 LIST_ROWS = 16
 X_BLOCKS = D // P
 DY_BLOCKS = DV // P
-EARLY = PASSES - 1
+MID = 2
 LAST = PASSES - 1
+VECTOR_PASSES = (3, 3, 2, 2)
+FORM_ORDER = (2, 3, 0, 1)
 CHUNKS = K_PASS // P
 TURN_BANKS = 8 - X_BLOCKS
 
@@ -40,19 +42,24 @@ def tile_attend_gmw_sig_kernel(tc, xT, dyT, hE, sw, tw, offs, offs2, out):
         dst = keep.tile([P, E // LIST_ROWS], U16, name="dst")
         x_tab = [keep.tile([P, V], F32, name="x_tab%d" % b) for b in range(X_BLOCKS)]
         dy_tab = [keep.tile([P, V], F32, name="dy_tab%d" % b) for b in range(DY_BLOCKS)]
-        h_early = [keep.tile([P, EARLY * K_PASS], F32, name="h_early%d" % b) for b in range(DY_BLOCKS)]
+        h_early = [keep.tile([P, VECTOR_PASSES[b] * K_PASS], F32, name="h_early%d" % b) for b in range(DY_BLOCKS)]
+        h_mid = keep.tile([P, 2, K_PASS], F32, name="h_mid")
+        square_mid = keep.tile([P, 2, K_PASS], F32, name="square_mid")
+        mid_turned = [keep.tile([P, 2 * P], F32, name="mid_turned%d" % c) for c in range(CHUNKS)]
+        mid_factor = [keep.tile([P, K_PASS], F32, name="mid_factor%d" % i) for i in range(2)]
+        dz_mid = [keep.tile([P, K_PASS], F32, name="dz_mid%d" % i) for i in range(2)]
         h_last = [keep.tile([P, 2, K_PASS], F32, name="h_last%d" % j) for j in range(2)]
         sw_in = [keep.tile([P, K_PASS], F32, name="sw_in%d" % g) for g in range(PASSES)]
-        tw_in = [keep.tile([P, K_PASS], F32, name="tw_in%d" % g) for g in range(EARLY)]
+        tw_in = [keep.tile([P, K_PASS], F32, name="tw_in%d" % g) for g in range(LAST)]
         tw_rows = keep.tile([P, P], F32, name="tw_rows")
-        tw_col = keep.tile([P, CHUNKS], F32, name="tw_col")
-        tw_bias = keep.tile([P, CHUNKS], F32, name="tw_bias")
+        tw_col = keep.tile([P, 2 * CHUNKS], F32, name="tw_col")
+        tw_bias = keep.tile([P, 2 * CHUNKS], F32, name="tw_bias")
         ident = keep.tile([P, P], F32, name="ident")
         xe_first = [keep.tile([P, K_PASS], F32, name="xe_first%d" % g) for g in range(PASSES)]
-        weighted = [keep.tile([P, EARLY * K_PASS], F32, name="weighted%d" % b) for b in range(DY_BLOCKS)]
+        weighted = [keep.tile([P, VECTOR_PASSES[b] * K_PASS], F32, name="weighted%d" % b) for b in range(DY_BLOCKS)]
         dz_last = [keep.tile([P, K_PASS], F32, name="dz_last%d" % b) for b in range(DY_BLOCKS)]
-        square_early = [keep.tile([P, EARLY * K_PASS], F32, name="square_early%d" % b) for b in range(DY_BLOCKS)]
-        dz_early = [keep.tile([P, EARLY * K_PASS], BF16, name="dz_early%d" % b) for b in range(DY_BLOCKS)]
+        square_early = [keep.tile([P, VECTOR_PASSES[b] * K_PASS], F32, name="square_early%d" % b) for b in range(DY_BLOCKS)]
+        dz_early = [keep.tile([P, VECTOR_PASSES[b] * K_PASS], BF16, name="dz_early%d" % b) for b in range(DY_BLOCKS)]
         square_last = [keep.tile([P, 2, K_PASS], F32, name="square_last%d" % j) for j in range(2)]
         factor_turned = [keep.tile([P, DV], F32, name="factor_turned%d" % c) for c in range(CHUNKS)]
         factor = [keep.tile([P, K_PASS], F32, name="factor%d" % b) for b in range(DY_BLOCKS)]
@@ -78,37 +85,39 @@ def tile_attend_gmw_sig_kernel(tc, xT, dyT, hE, sw, tw, offs, offs2, out):
 
         xe = {(0, g): xe_first[g][:] for g in range(PASSES)}
         for j in range(2):
-            xe[1, j] = weighted[DY_BLOCKS - 1][:, edges(j)]
+            xe[1, j] = weighted[FORM_ORDER[2 + j]][:, edges(0)]
             xe[1, 2 + j] = dz_woven[j][:, 0, 0 : 2 * K_PASS].bitcast(F32)
 
         def load_h_last(j):
             nc.sync.dma_start(h_last[j][:], hE[2 * j * P : 2 * (j + 1) * P, edges(LAST)].rearrange("(b p) e -> p b e", p=P))
 
         def load_h_early(b):
-            nc.sync.dma_start(h_early[b][:], hE[run(b), 0 : EARLY * K_PASS])
+            nc.sync.dma_start(h_early[b][:], hE[run(b), 0 : VECTOR_PASSES[b] * K_PASS])
 
         def load_dy(b):
             nc.sync.dma_start(dy_tab[b][:], dyT[run(b), :])
 
         nc.gpsimd.memset(tw_rows[:], 0.0)
         make_identity(nc, ident[:])
-        nc.sync.dma_start(src[:], offs)
-        nc.sync.dma_start(x_tab[0][:], xT[run(0), :])
-        for j in range(2):
-            nc.sync.dma_start(sw_in[0][:, half(j)], sw[:, half(j)])
-        nc.scalar.dma_start(tw_rows[0:CHUNKS, :], tw[0:1, edges(LAST)].rearrange("o (c p) -> (o c) p", p=P))
-        for g in range(1, PASSES):
-            nc.sync.dma_start(sw_in[g][:], sw[:, edges(g)])
         nc.sync.dma_start(dst[:], offs2)
         load_dy(0)
-        for g in range(EARLY):
+        for j in range(2):
+            nc.sync.dma_start(tw_in[0][:, half(j)], tw[:, half(j)])
+        nc.scalar.dma_start(tw_rows[0 : 2 * CHUNKS, :], tw[0:1, MID * K_PASS : E].rearrange("o (c p) -> (o c) p", p=P))
+        for g in range(1, LAST):
             nc.sync.dma_start(tw_in[g][:], tw[:, edges(g)])
+        load_dy(1)
         for j in range(2):
             load_h_last(j)
-            load_dy(1 + j)
-        load_h_early(0)
-        load_dy(DY_BLOCKS - 1)
-        for b in range(1, DY_BLOCKS):
+        for b in range(2, DY_BLOCKS):
+            load_dy(b)
+        nc.sync.dma_start(h_mid[:], hE[2 * P : 4 * P, edges(MID)].rearrange("(b p) e -> p b e", p=P))
+        load_h_early(FORM_ORDER[0])
+        nc.sync.dma_start(src[:], offs)
+        nc.sync.dma_start(x_tab[0][:], xT[run(0), :])
+        for g in range(PASSES):
+            nc.sync.dma_start(sw_in[g][:], sw[:, edges(g)])
+        for b in FORM_ORDER[1:]:
             load_h_early(b)
         nc.sync.dma_start(x_tab[1][:], xT[run(1), :])
 
@@ -170,8 +179,8 @@ def tile_attend_gmw_sig_kernel(tc, xT, dyT, hE, sw, tw, offs, offs2, out):
         def tw_columns():
             bank = next_bank()
             nc.tensor.transpose(bank[:, 0, :], tw_rows[:], ident[:])
-            nc.scalar.copy(tw_col[:], bank[:, 0, 0:CHUNKS])
-            nc.scalar.activation(tw_bias[:], bank[:, 0, 0:CHUNKS], ACT.Copy, scale=-0.25)
+            nc.scalar.copy(tw_col[:], bank[:, 0, 0 : 2 * CHUNKS])
+            nc.scalar.activation(tw_bias[:], bank[:, 0, 0 : 2 * CHUNKS], ACT.Copy, scale=-0.25)
 
         def square(target, h):
             nc.scalar.activation(target[:], h[:], ACT.Square, bias=-0.5, scale=1.0)
@@ -184,8 +193,8 @@ def tile_attend_gmw_sig_kernel(tc, xT, dyT, hE, sw, tw, offs, offs2, out):
                 factor_turned[c][:],
                 bank[:].rearrange("p b n -> p (b n)"),
                 ACT.Identity,
-                bias=tw_bias[:, c : c + 1],
-                scale=tw_col[:, c : c + 1],
+                bias=tw_bias[:, CHUNKS + c : CHUNKS + c + 1],
+                scale=tw_col[:, CHUNKS + c : CHUNKS + c + 1],
             )
 
         def factor_turn_back(b):
@@ -193,6 +202,33 @@ def tile_attend_gmw_sig_kernel(tc, xT, dyT, hE, sw, tw, offs, offs2, out):
             for c in range(CHUNKS):
                 nc.tensor.transpose(bank[:, c, :], factor_turned[c][:, run(b)], ident[:])
             nc.scalar.copy(factor[b][:], bank[:].rearrange("p c e -> p (c e)"))
+
+        def mid_scale(j):
+            bank = next_bank()
+            for i in range(2):
+                for b in range(2):
+                    nc.tensor.transpose(bank[:, 2 * i + b, :], square_mid[:, b, run(2 * j + i)], ident[:])
+            for i in range(2):
+                c = 2 * j + i
+                nc.scalar.activation(
+                    mid_turned[c][:],
+                    bank[:, 2 * i : 2 * i + 2, :].rearrange("p b n -> p (b n)"),
+                    ACT.Identity,
+                    bias=tw_bias[:, c : c + 1],
+                    scale=tw_col[:, c : c + 1],
+                )
+
+        def mid_turn_back(i):
+            bank = next_bank()
+            for c in range(CHUNKS):
+                nc.tensor.transpose(bank[:, c, :], mid_turned[c][:, run(i)], ident[:])
+            nc.scalar.copy(mid_factor[i][:], bank[:].rearrange("p c e -> p (c e)"))
+
+        def mid_gather(i):
+            gather(dz_mid[i][:], dy_tab[2 + i], dst, MID * K_PASS, mid_factor[i][:])
+
+        def mid_weave(i):
+            weave(dz_mid[i], dz_woven[MID // 2][:, MID % 2, (2 + i) * K_PASS : (3 + i) * K_PASS])
 
         def last_gather(b):
             gather(dz_last[b][:], dy_tab[b], dst, LAST * K_PASS, factor[b][:])
@@ -220,13 +256,13 @@ def tile_attend_gmw_sig_kernel(tc, xT, dyT, hE, sw, tw, offs, offs2, out):
                 bank[:].rearrange("p (g u) n -> p g n u", u=2),
             )
 
-        def early_weave_2(j):
+        def early_weave_2():
             bank = next_bank()
-            for i in range(2):
-                turn_pairs(bank, i, 2 * j + i, 2)
+            for b in range(2):
+                turn_pairs(bank, b, b, MID)
             nc.scalar.copy(
-                dz_woven[1][:, 0, 2 * j * K_PASS : 2 * (j + 1) * K_PASS].bitcast(F32).rearrange("p (i n u) -> p i n u", i=2, u=2),
-                bank[:].rearrange("p (i u) n -> p i n u", u=2),
+                dz_woven[MID // 2][:, MID % 2, 0 : 2 * K_PASS].bitcast(F32).rearrange("p (b n u) -> p b n u", b=2, u=2),
+                bank[:].rearrange("p (b u) n -> p b n u", u=2),
             )
 
         def product(b, g):
@@ -243,54 +279,67 @@ def tile_attend_gmw_sig_kernel(tc, xT, dyT, hE, sw, tw, offs, offs2, out):
 
         tw_columns()
         for j in range(2):
-            gather(xe[0, 0][:, half(j)], x_tab[0], src, half(j).start, sw_in[0][:, half(j)])
-        for g in range(1, PASSES):
-            x_gather(0, g)
-        for g in range(LAST):
-            x_weave(0, g)
+            gather(weighted[0][:, half(j)], dy_tab[0], dst, half(j).start, tw_in[0][:, half(j)])
         for b in range(DY_BLOCKS):
-            for g in range(EARLY):
+            for g in range(1 if b == 0 else 0, VECTOR_PASSES[b]):
                 early_gather(b, g)
+
         for j in range(2):
             square(square_last[j], h_last[j])
         for c in range(CHUNKS):
             factor_scale(c)
-        square(square_early[0], h_early[0])
-        for b in range(2):
+        square(square_mid, h_mid)
+        for b in range(DY_BLOCKS):
             factor_turn_back(b)
-        x_weave(0, LAST)
-        for b in range(2, DY_BLOCKS):
-            factor_turn_back(b)
-        for b in range(1, DY_BLOCKS):
-            square(square_early[b], h_early[b])
-        x_quantise(0, 0, PASSES)
         for b in range(DY_BLOCKS):
             last_gather(b)
-            early_form(b)
-        for b in range(DY_BLOCKS):
+        square(square_early[FORM_ORDER[0]], h_early[FORM_ORDER[0]])
+        early_form(FORM_ORDER[0])
+        for j in range(2):
+            mid_scale(j)
+        last_weave(0)
+        for i in range(2):
+            mid_turn_back(i)
+
+        for g in range(PASSES):
+            x_gather(0, g)
+        for b in range(1, DY_BLOCKS):
             last_weave(b)
+        for i in range(2):
+            mid_gather(i)
+        square(square_early[FORM_ORDER[1]], h_early[FORM_ORDER[1]])
+        for g in range(PASSES):
+            x_weave(0, g)
+        for b in FORM_ORDER[2:]:
+            square(square_early[b], h_early[b])
+        for b in FORM_ORDER[1:]:
+            early_form(b)
+        x_quantise(0, 0, PASSES)
+        for i in range(2):
+            mid_weave(i)
+        for b in FORM_ORDER:
             early_weave_01(b)
-            if b % 2:
-                early_weave_2(b // 2)
+        early_weave_2()
+
         x_gather(1, 0)
         x_gather(1, 1)
         x_weave(1, 0)
-        dz_quantise(0, 2)
-        dz_quantise(2, 3)
+        dz_quantise(0, MID)
+        dz_quantise(MID, LAST)
         x_weave(1, 1)
-        x_gather(1, 2)
-        for g in range(EARLY):
+        x_gather(1, MID)
+        for g in range(LAST):
             product(0, g)
-        x_quantise(1, 0, 2)
-        x_weave(1, 2)
+        x_quantise(1, 0, MID)
+        x_weave(1, MID)
         x_gather(1, LAST)
-        for g in range(2):
+        for g in range(MID):
             product(1, g)
         x_weave_end()
         dz_quantise(LAST, PASSES)
-        x_quantise(1, 2, LAST)
+        x_quantise(1, MID, LAST)
         product(0, LAST)
-        product(1, 2)
+        product(1, MID)
         x_quantise_end()
         product(1, LAST)
 

from contextlib import ExitStack

import concourse.mybir as mybir
from concourse.masks import make_identity

V, E, D, DV = 1024, 2048, 256, 512
FLOPS = 2 * D * DV * E

F32 = mybir.dt.float32
BF16 = mybir.dt.bfloat16
U32 = mybir.dt.uint32
U16 = mybir.dt.uint16
U8 = mybir.dt.uint8
E4M3 = mybir.dt.float8_e4m3fn_x4
E5M2 = mybir.dt.float8_e5m2_x4
ACT = mybir.ActivationFunctionType
ALU = mybir.AluOpType

P = 128
PACK = 4
K_PASS = P * PACK
PASSES = E // K_PASS
PAIRS = K_PASS // 2
LIST_ROWS = 16
X_BLOCKS = D // P
DY_BLOCKS = DV // P
MID = 2
LAST = PASSES - 1
VECTOR_PASSES = (3, 3, 2, 2)
FORM_ORDER = (2, 3, 0, 1)
CHUNKS = K_PASS // P
TURN_BANKS = 8 - X_BLOCKS


def tile_attend_gmw_sig_kernel(tc, xT, dyT, hE, sw, tw, offs, offs2, out):
    nc = tc.nc
    with ExitStack() as ctx:
        keep = ctx.enter_context(tc.tile_pool(name="keep", bufs=1))
        psum = ctx.enter_context(tc.psum_pool(name="psum", bufs=1))

        src = keep.tile([P, E // LIST_ROWS], U16, name="src")
        dst = keep.tile([P, E // LIST_ROWS], U16, name="dst")
        x_tab = [keep.tile([P, V], F32, name="x_tab%d" % b) for b in range(X_BLOCKS)]
        dy_tab = [keep.tile([P, V], F32, name="dy_tab%d" % b) for b in range(DY_BLOCKS)]
        h_early = [keep.tile([P, VECTOR_PASSES[b] * K_PASS], F32, name="h_early%d" % b) for b in range(DY_BLOCKS)]
        h_mid = keep.tile([P, 2, K_PASS], F32, name="h_mid")
        square_mid = keep.tile([P, 2, K_PASS], F32, name="square_mid")
        mid_turned = [keep.tile([P, 2 * P], F32, name="mid_turned%d" % c) for c in range(CHUNKS)]
        mid_factor = [keep.tile([P, K_PASS], F32, name="mid_factor%d" % i) for i in range(2)]
        dz_mid = [keep.tile([P, K_PASS], F32, name="dz_mid%d" % i) for i in range(2)]
        h_last = [keep.tile([P, 2, K_PASS], F32, name="h_last%d" % j) for j in range(2)]
        sw_in = [keep.tile([P, K_PASS], F32, name="sw_in%d" % g) for g in range(PASSES)]
        tw_in = [keep.tile([P, K_PASS], F32, name="tw_in%d" % g) for g in range(LAST)]
        tw_rows = keep.tile([P, P], F32, name="tw_rows")
        tw_col = keep.tile([P, 2 * CHUNKS], F32, name="tw_col")
        tw_bias = keep.tile([P, 2 * CHUNKS], F32, name="tw_bias")
        ident = keep.tile([P, P], F32, name="ident")
        xe_first = [keep.tile([P, K_PASS], F32, name="xe_first%d" % g) for g in range(PASSES)]
        weighted = [keep.tile([P, VECTOR_PASSES[b] * K_PASS], F32, name="weighted%d" % b) for b in range(DY_BLOCKS)]
        dz_last = [keep.tile([P, K_PASS], F32, name="dz_last%d" % b) for b in range(DY_BLOCKS)]
        square_early = [keep.tile([P, VECTOR_PASSES[b] * K_PASS], F32, name="square_early%d" % b) for b in range(DY_BLOCKS)]
        dz_early = [keep.tile([P, VECTOR_PASSES[b] * K_PASS], BF16, name="dz_early%d" % b) for b in range(DY_BLOCKS)]
        square_last = [keep.tile([P, 2, K_PASS], F32, name="square_last%d" % j) for j in range(2)]
        factor_turned = [keep.tile([P, DV], F32, name="factor_turned%d" % c) for c in range(CHUNKS)]
        factor = [keep.tile([P, K_PASS], F32, name="factor%d" % b) for b in range(DY_BLOCKS)]
        result = [keep.tile([P, DV], F32, name="result%d" % b) for b in range(X_BLOCKS)]
        x_woven = [keep.tile([P, PASSES - b, K_PASS], BF16, name="x_woven%d" % b, align_bytes=64) for b in range(X_BLOCKS)]
        x_codes = [keep.tile([P, PASSES * P], U32, name="x_codes%d" % b, align_bytes=64) for b in range(X_BLOCKS)]
        x_scales = [keep.tile([P, PASSES * P], U8, name="x_scales%d" % b, align_bytes=64) for b in range(X_BLOCKS)]
        x_end_woven = keep.tile([P, K_PASS], BF16, name="x_end_woven", align_bytes=64)
        dz_woven = [keep.tile([P, 2, DV * PACK], BF16, name="dz_woven%d" % j, align_bytes=64) for j in range(2)]
        dz_codes = [keep.tile([P, 2 * DV], U32, name="dz_codes%d" % j, align_bytes=64) for j in range(2)]
        dz_scales = [keep.tile([P, 2 * DV], U8, name="dz_scales%d" % j, align_bytes=64) for j in range(2)]
        banks = [psum.tile([P, PACK, P], F32, name="bank%d" % i) for i in range(TURN_BANKS)]
        sums = [psum.tile([P, DV], F32, name="sums%d" % b) for b in range(X_BLOCKS)]

        def edges(g):
            return slice(g * K_PASS, (g + 1) * K_PASS)

        def half(j):
            return slice(j * K_PASS // 2, (j + 1) * K_PASS // 2)

        def run(i):
            return slice(i * P, (i + 1) * P)

        xe = {(0, g): xe_first[g][:] for g in range(PASSES)}
        for j in range(2):
            xe[1, j] = weighted[FORM_ORDER[2 + j]][:, edges(0)]
            xe[1, 2 + j] = dz_woven[j][:, 0, 0 : 2 * K_PASS].bitcast(F32)

        def load_h_last(j):
            nc.sync.dma_start(h_last[j][:], hE[2 * j * P : 2 * (j + 1) * P, edges(LAST)].rearrange("(b p) e -> p b e", p=P))

        def load_h_early(b):
            nc.sync.dma_start(h_early[b][:], hE[run(b), 0 : VECTOR_PASSES[b] * K_PASS])

        def load_dy(b):
            nc.sync.dma_start(dy_tab[b][:], dyT[run(b), :])

        nc.gpsimd.memset(tw_rows[:], 0.0)
        make_identity(nc, ident[:])
        nc.sync.dma_start(dst[:], offs2)
        load_dy(0)
        for j in range(2):
            nc.sync.dma_start(tw_in[0][:, half(j)], tw[:, half(j)])
        nc.scalar.dma_start(tw_rows[0 : 2 * CHUNKS, :], tw[0:1, MID * K_PASS : E].rearrange("o (c p) -> (o c) p", p=P))
        for g in range(1, LAST):
            nc.sync.dma_start(tw_in[g][:], tw[:, edges(g)])
        load_dy(1)
        for j in range(2):
            load_h_last(j)
        for b in range(2, DY_BLOCKS):
            load_dy(b)
        nc.sync.dma_start(h_mid[:], hE[2 * P : 4 * P, edges(MID)].rearrange("(b p) e -> p b e", p=P))
        load_h_early(FORM_ORDER[0])
        nc.sync.dma_start(src[:], offs)
        nc.sync.dma_start(x_tab[0][:], xT[run(0), :])
        for g in range(PASSES):
            nc.sync.dma_start(sw_in[g][:], sw[:, edges(g)])
        for b in FORM_ORDER[1:]:
            load_h_early(b)
        nc.sync.dma_start(x_tab[1][:], xT[run(1), :])

        taken = []

        def next_bank():
            taken.append(len(taken) % TURN_BANKS)
            return banks[taken[-1]]

        def gather(target, table, offsets, first_edge, scale):
            columns = slice(first_edge // LIST_ROWS, (first_edge + target.shape[1]) // LIST_ROWS)
            nc.vector.tensor_tensor(target, table[:].indirect(offsets[:, columns]), scale, ALU.mult)

        def weave(values, target):
            bank = next_bank()
            for t in range(PACK):
                nc.tensor.transpose(bank[:, t, :], values[:, t:K_PASS:PACK], ident[:])
            nc.scalar.copy(target.rearrange("p (c t) -> p c t", t=PACK), bank[:].rearrange("p t c -> p c t"))

        def x_gather(b, g):
            gather(xe[b, g], x_tab[b], src, g * K_PASS, sw_in[g][:])

        def x_weave(b, g):
            weave(xe[b, g], x_woven[b][:, g, :])

        def x_weave_end():
            words = result[0][:, 0:PAIRS]
            nc.vector.tensor_copy(
                words.bitcast(BF16).rearrange("p (u s j) -> p u s j", u=2, j=2),
                xe[1, LAST].rearrange("p (s u j) -> p u s j", u=2, j=2),
            )
            bank = next_bank()
            for u in range(2):
                nc.tensor.transpose(bank[:, u, :], words[:, run(u)], ident[:])
            nc.scalar.copy(
                x_end_woven[:].bitcast(F32).rearrange("p (n u) -> p n u", u=2),
                bank[:, 0:2, :].rearrange("p u n -> p n u"),
            )

        def x_quantise(b, first, end):
            nc.vector.quantize_mx(
                out=x_codes[b][:, first * P : end * P].bitcast(E4M3),
                scales=x_scales[b][:, first * P : end * P],
                in_=x_woven[b][:, first:end, :].rearrange("p g c -> p (g c)"),
            )

        def x_quantise_end():
            nc.vector.quantize_mx(out=x_codes[1][:, run(LAST)].bitcast(E4M3), scales=x_scales[1][:, run(LAST)], in_=x_end_woven[:])

        def dz_quantise(first, end):
            j, i = divmod(first, 2)
            count = end - first
            nc.vector.quantize_mx(
                out=dz_codes[j][:, i * DV : (i + count) * DV].bitcast(E5M2),
                scales=dz_scales[j][:, i * DV : (i + count) * DV],
                in_=dz_woven[j][:, i : i + count, :].rearrange("p g c -> p (g c)"),
            )

        def tw_columns():
            bank = next_bank()
            nc.tensor.transpose(bank[:, 0, :], tw_rows[:], ident[:])
            nc.scalar.copy(tw_col[:], bank[:, 0, 0 : 2 * CHUNKS])
            nc.scalar.activation(tw_bias[:], bank[:, 0, 0 : 2 * CHUNKS], ACT.Copy, scale=-0.25)

        def square(target, h):
            nc.scalar.activation(target[:], h[:], ACT.Square, bias=-0.5, scale=1.0)

        def factor_scale(c):
            bank = next_bank()
            for b in range(DY_BLOCKS):
                nc.tensor.transpose(bank[:, b, :], square_last[b // 2][:, b % 2, run(c)], ident[:])
            nc.scalar.activation(
                factor_turned[c][:],
                bank[:].rearrange("p b n -> p (b n)"),
                ACT.Identity,
                bias=tw_bias[:, CHUNKS + c : CHUNKS + c + 1],
                scale=tw_col[:, CHUNKS + c : CHUNKS + c + 1],
            )

        def factor_turn_back(b):
            bank = next_bank()
            for c in range(CHUNKS):
                nc.tensor.transpose(bank[:, c, :], factor_turned[c][:, run(b)], ident[:])
            nc.scalar.copy(factor[b][:], bank[:].rearrange("p c e -> p (c e)"))

        def mid_scale(j):
            bank = next_bank()
            for i in range(2):
                for b in range(2):
                    nc.tensor.transpose(bank[:, 2 * i + b, :], square_mid[:, b, run(2 * j + i)], ident[:])
            for i in range(2):
                c = 2 * j + i
                nc.scalar.activation(
                    mid_turned[c][:],
                    bank[:, 2 * i : 2 * i + 2, :].rearrange("p b n -> p (b n)"),
                    ACT.Identity,
                    bias=tw_bias[:, c : c + 1],
                    scale=tw_col[:, c : c + 1],
                )

        def mid_turn_back(i):
            bank = next_bank()
            for c in range(CHUNKS):
                nc.tensor.transpose(bank[:, c, :], mid_turned[c][:, run(i)], ident[:])
            nc.scalar.copy(mid_factor[i][:], bank[:].rearrange("p c e -> p (c e)"))

        def mid_gather(i):
            gather(dz_mid[i][:], dy_tab[2 + i], dst, MID * K_PASS, mid_factor[i][:])

        def mid_weave(i):
            weave(dz_mid[i], dz_woven[MID // 2][:, MID % 2, (2 + i) * K_PASS : (3 + i) * K_PASS])

        def last_gather(b):
            gather(dz_last[b][:], dy_tab[b], dst, LAST * K_PASS, factor[b][:])

        def last_weave(b):
            weave(dz_last[b], dz_woven[LAST // 2][:, LAST % 2, b * K_PASS : (b + 1) * K_PASS])

        def early_gather(b, g):
            gather(weighted[b][:, edges(g)], dy_tab[b], dst, g * K_PASS, tw_in[g][:])

        def early_form(b):
            nc.vector.scalar_tensor_tensor(dz_early[b][:], square_early[b][:], 0.25, weighted[b][:], ALU.subtract, ALU.mult)

        def turn_pairs(bank, place, b, g):
            words = dz_early[b][:].bitcast(F32)
            for u in range(2):
                nc.tensor.transpose(bank[:, 2 * place + u, :], words[:, PAIRS * g + u : PAIRS * (g + 1) : 2], ident[:])

        def early_weave_01(b):
            bank = next_bank()
            for g in range(2):
                turn_pairs(bank, g, b, g)
            nc.scalar.copy(
                dz_woven[0][:, :, b * K_PASS : (b + 1) * K_PASS].bitcast(F32).rearrange("p g (n u) -> p g n u", u=2),
                bank[:].rearrange("p (g u) n -> p g n u", u=2),
            )

        def early_weave_2():
            bank = next_bank()
            for b in range(2):
                turn_pairs(bank, b, b, MID)
            nc.scalar.copy(
                dz_woven[MID // 2][:, MID % 2, 0 : 2 * K_PASS].bitcast(F32).rearrange("p (b n u) -> p b n u", b=2, u=2),
                bank[:].rearrange("p (b u) n -> p b n u", u=2),
            )

        def product(b, g):
            j, i = divmod(g, 2)
            nc.tensor.matmul_mx(
                out=sums[b][:],
                lhsT=x_codes[b][:, run(g)].bitcast(E4M3),
                lhsT_scale=x_scales[b][:, run(g)],
                rhs=dz_codes[j][:, i * DV : (i + 1) * DV].bitcast(E5M2),
                rhs_scale=dz_scales[j][:, i * DV : (i + 1) * DV],
                start=(g == 0),
                stop=(g == LAST),
            )

        tw_columns()
        for j in range(2):
            gather(weighted[0][:, half(j)], dy_tab[0], dst, half(j).start, tw_in[0][:, half(j)])
        for b in range(DY_BLOCKS):
            for g in range(1 if b == 0 else 0, VECTOR_PASSES[b]):
                early_gather(b, g)

        for j in range(2):
            square(square_last[j], h_last[j])
        for c in range(CHUNKS):
            factor_scale(c)
        square(square_mid, h_mid)
        for b in range(DY_BLOCKS):
            factor_turn_back(b)
        for b in range(DY_BLOCKS):
            last_gather(b)
        square(square_early[FORM_ORDER[0]], h_early[FORM_ORDER[0]])
        early_form(FORM_ORDER[0])
        for j in range(2):
            mid_scale(j)
        last_weave(0)
        for i in range(2):
            mid_turn_back(i)

        for g in range(PASSES):
            x_gather(0, g)
        for b in range(1, DY_BLOCKS):
            last_weave(b)
        for i in range(2):
            mid_gather(i)
        square(square_early[FORM_ORDER[1]], h_early[FORM_ORDER[1]])
        for g in range(PASSES):
            x_weave(0, g)
        for b in FORM_ORDER[2:]:
            square(square_early[b], h_early[b])
        for b in FORM_ORDER[1:]:
            early_form(b)
        x_quantise(0, 0, PASSES)
        for i in range(2):
            mid_weave(i)
        for b in FORM_ORDER:
            early_weave_01(b)
        early_weave_2()

        x_gather(1, 0)
        x_gather(1, 1)
        x_weave(1, 0)
        dz_quantise(0, MID)
        dz_quantise(MID, LAST)
        x_weave(1, 1)
        x_gather(1, MID)
        for g in range(LAST):
            product(0, g)
        x_quantise(1, 0, MID)
        x_weave(1, MID)
        x_gather(1, LAST)
        for g in range(MID):
            product(1, g)
        x_weave_end()
        dz_quantise(LAST, PASSES)
        x_quantise(1, MID, LAST)
        product(0, LAST)
        product(1, MID)
        x_quantise_end()
        product(1, LAST)

        nc.scalar.activation(result[0][:], sums[0][:], ACT.Copy, scale=-1.0)
        nc.sync.dma_start(out[run(0), :], result[0][:])
        for j, queue in enumerate((nc.sync, nc.scalar)):
            cols = slice(j * DV // 2, (j + 1) * DV // 2)
            nc.vector.tensor_scalar(result[1][:, cols], sums[1][:, cols], -1.0, None, ALU.mult)
            queue.dma_start(out[run(1), cols], result[1][:, cols])
